import numpy as np
import ml_dtypes


def mxq(x, axis, fmt="e4m3"):
    dtype, down = {"e4m3": (ml_dtypes.float8_e4m3fn, 7), "e5m2": (ml_dtypes.float8_e5m2, 14)}[fmt]
    v = np.moveaxis(np.asarray(x, np.float32).astype(ml_dtypes.bfloat16).astype(np.float64), axis, -1)
    blocks = v.reshape(v.shape[:-1] + (-1, 32))
    amax = np.abs(blocks).max(-1, keepdims=True)
    byte = np.maximum(np.where(amax > 0, np.frexp(amax)[1] - 1 + 127, 0) - down, 1)
    scale = np.exp2(byte - 127.0)
    codes = (blocks / scale).astype(np.float32).astype(dtype).astype(np.float64)
    return np.moveaxis((codes * scale).reshape(v.shape), -1, axis)


WIDE = False


def mx_kscale(k):
    if not WIDE:
        return np.ones(k)
    levels = np.array([10, -10, 5, -5, 0])
    if k % 512:
        return np.exp2(np.random.permutation(np.resize(levels, k // 32))).repeat(32)
    a = np.empty((k // 512, 16))
    for p in range(k // 512):
        a[p, :8] = np.random.permutation(np.resize(levels, 8))
        for g in range(8):
            far = levels[np.abs(levels - a[p, g]) >= 10]
            a[p, g + 8] = far[np.random.randint(len(far))]
    return np.exp2(a.ravel()).repeat(32)


BF16 = ml_dtypes.bfloat16


def bf(x):
    return np.asarray(x, np.float32).astype(BF16)


def f64(x):
    return np.asarray(x).astype(np.float64)


E2M1 = np.array([0.0, 0.5, 1.0, 1.5, 2.0, 3.0, 4.0, 6.0, -0.0, -0.5, -1.0, -1.5, -2.0, -3.0, -4.0, -6.0])


def pack_weight(w, fmt):
    k, n = w.shape
    w = f64(bf(w)).reshape(k // 32, 32, n)
    amax = np.abs(w).max(1)
    if fmt == "e4m3":
        byte = np.frexp(amax)[1] - 1 + 127 - 7
    else:
        mant, ex = np.frexp(amax / 6.0)
        byte = np.where(mant > 0.5, ex, ex - 1) + 127
    byte = np.clip(np.where(amax > 0, byte, 1), 1, 254)
    scaled = (w * np.exp2(127.0 - byte)[:, None, :]).reshape(k, n).astype(np.float32)
    by_word = np.ascontiguousarray(scaled.reshape(k // 512, 128, 4, n).transpose(0, 1, 3, 2))
    if fmt == "e4m3":
        words = by_word.astype(ml_dtypes.float8_e4m3fn).view(np.uint8)
    else:
        c = by_word.astype(ml_dtypes.float4_e2m1fn).view(np.uint8) & 0xF
        words = c[..., 0::2] | (c[..., 1::2] << 4)
    return np.ascontiguousarray(words), np.ascontiguousarray(byte.astype(np.uint8).reshape(k // 512, 16, n))


def unpack_weight(words, scales, fmt):
    g, p, n, _ = words.shape
    if fmt == "e4m3":
        vals = np.ascontiguousarray(words).view(ml_dtypes.float8_e4m3fn).astype(np.float64)
    else:
        nib = np.empty((g, p, n, 4), np.uint8)
        nib[..., 0::2] = words & 0xF
        nib[..., 1::2] = words >> 4
        vals = E2M1[nib]
    vals = vals * np.repeat(np.exp2(scales.astype(np.float64) - 127.0), 8, axis=1)[..., None]
    return vals.transpose(0, 1, 3, 2).reshape(g * 512, n)
def pack4(w):
    words, scales = pack_weight(w, "e2m1")
    return words.reshape(words.shape[0], 128, -1), scales


def unpack4(words, scales):
    return unpack_weight(words.reshape(words.shape[0], 128, -1, 2), scales, "e2m1")


M, K, N, D, V = 768, 1536, 1024, 512, 128

EPS = 1e-3
ROOT_HALF = np.sqrt(0.5)


def sigmoid(v):
    return 0.5 * (1.0 + np.tanh(0.5 * v))


def ghost_norm(u, gain, shift):
    v = u.reshape(M // V, V, 2 * N)
    c = v - v.mean(axis=1, keepdims=True)
    var = (c * c).mean(axis=1, keepdims=True)
    return (c / np.sqrt(var + EPS)).reshape(M, 2 * N) * gain + shift


def setup_inputs():
    s, t = mx_kscale(K), mx_kscale(N)
    tt = np.concatenate([np.ones(N), t])
    x = np.random.standard_normal((K, M)) + 0.5 * np.random.standard_normal((K, 1))
    a = np.random.standard_normal((K, 2 * N)) / np.sqrt(K)
    b = np.random.standard_normal((N, 2 * N)) / np.sqrt(N)
    xt_words, xt_scales = pack4(x * s[:, None])
    a_words, a_scales = pack4(a / s[:, None])
    b_words, b_scales = pack4(b / t[:, None])
    return {"xt_words": xt_words, "xt_scales": xt_scales,
            "a_words": a_words, "a_scales": a_scales,
            "b_words": b_words, "b_scales": b_scales,
            "gain1": bf((1.0 + 0.1 * np.random.standard_normal(2 * N)) * tt),
            "shift1": bf(0.3 * np.random.standard_normal(2 * N) * tt),
            "gain2": bf(1.0 + 0.1 * np.random.standard_normal(2 * N)),
            "shift2": bf(0.3 * np.random.standard_normal(2 * N)),
            "skip": bf((1.0 + 0.1 * np.random.standard_normal(N)) / t),
            "d_prev": bf(0.5 * np.abs(np.random.standard_normal((M, D))))}


def reference(xt_words, xt_scales, a_words, a_scales, b_words, b_scales, gain1, shift1, gain2, shift2, skip, d_prev):
    u = unpack4(xt_words, xt_scales).T @ unpack4(a_words, a_scales)
    u = ghost_norm(u, f64(gain1), f64(shift1))
    h = sigmoid(u[:, :N]) * u[:, N:]
    z = mxq(h, 1, "e4m3") @ unpack4(b_words, b_scales)
    z = ghost_norm(z, f64(gain2), f64(shift2))
    y = (sigmoid(z[:, :N]) * z[:, N:] + h * f64(skip)) * ROOT_HALF
    decision = f64(d_prev) + np.maximum(y[:, :D], 0.0)
    attention = y[:, D:]
    return decision, attention

@@ -1,0 +1,326 @@
+from contextlib import ExitStack
+
+import concourse.mybir as mybir
+from concourse.masks import make_identity
+
+M, K, N, D, V = 768, 1536, 1024, 512, 128
+EPS = 1e-3
+ROOT_HALF = 0.5**0.5
+
+FLOPS = 2 * M * K * 2 * N + 2 * M * N * 2 * N
+
+F32 = mybir.dt.float32
+BF16 = mybir.dt.bfloat16
+I32 = mybir.dt.int32
+U32 = mybir.dt.uint32
+U8 = mybir.dt.uint8
+FP8X4 = mybir.dt.float8_e4m3fn_x4
+FP4X4 = mybir.dt.float4_e2m1fn_x4
+ADD = mybir.AluOpType.add
+MULT = mybir.AluOpType.mult
+SUB = mybir.AluOpType.subtract
+MAX = mybir.AluOpType.max
+POW = mybir.AluOpType.pow
+SIGMOID = mybir.ActivationFunctionType.Sigmoid
+IDENTITY = mybir.ActivationFunctionType.Identity
+
+P = 128
+GK = K // 512
+GN = N // 512
+
+
+def tile_tabnet_glu_step_f2_kernel(
+    tc, xt_words, xt_scales, a_words, a_scales, b_words, b_scales,
+    gain1, shift1, gain2, shift2, skip, d_prev, out_0, out_1,
+):
+    nc = tc.nc
+    with ExitStack() as ctx:
+        keep = ctx.enter_context(tc.tile_pool(name="keep", bufs=1))
+        work = ctx.enter_context(tc.tile_pool(name="work", bufs=3))
+        psum = ctx.enter_context(tc.psum_pool(name="psum", bufs=6))
+        ctx.enter_context(tc.manual_schedule())
+
+        xt_w = keep.tile([P, GK, 2 * M], U8, align_bytes=64, name="xt_w")
+        xt_s = keep.tile([P, GK, M], U8, align_bytes=64, name="xt_s")
+        a_w = keep.tile([P, GK, 4 * N], U8, align_bytes=64, name="a_w")
+        a_s = keep.tile([P, GK, 2 * N], U8, align_bytes=64, name="a_s")
+        b_w = keep.tile([P, GN, 4 * N], U8, align_bytes=64, name="b_w")
+        b_s = keep.tile([P, GN, 2 * N], U8, align_bytes=64, name="b_s")
+        vec_in = keep.tile([P, P], BF16, name="vec_in")
+        vec_in32 = keep.tile([P, P], F32, name="vec_in32")
+        vec = keep.tile([P, P], F32, name="vec")
+        ident = keep.tile([P, P], F32, name="ident")
+        neg_half = keep.tile([P, 8], F32, name="neg_half")
+        warm = keep.tile([P, 1], F32, name="warm")
+        dp = keep.tile([P, M // V, D], BF16, name="dp")
+        h_all = keep.tile([P, N // P, M], F32, name="h_all")
+        hc = keep.tile([P, GN, M], U32, align_bytes=64, name="hc")
+        hs = keep.tile([P, GN, M], U8, align_bytes=64, name="hs")
+
+        nc.vector.memset(xt_s[:].rearrange("p g n -> p (g n)").bitcast(I32), 0)
+        nc.vector.memset(a_s[:].rearrange("p g n -> p (g n)").bitcast(I32), 0)
+        nc.vector.memset(vec_in[:], 0.0)
+        nc.vector.memset(b_s[:].rearrange("p g n -> p (g n)").bitcast(I32), 0)
+        nc.gpsimd.memset(warm[:], 0.0)
+        nc.gpsimd.memset(neg_half[:], -0.5)
+        make_identity(nc, ident[:])
+        nc.scalar.activation(out=warm[:], in_=warm[:], func=SIGMOID)
+
+        def load_scales(plane, src):
+            for q in range(4):
+                nc.sync.dma_start(
+                    out=plane[32 * q : 32 * q + 4, :, :].bitcast(I32),
+                    in_=src[:, 4 * q : 4 * q + 4, :].rearrange("g q n -> q g n").bitcast(I32),
+                )
+
+        def load_words(tile, src, c0, c1):
+            nc.sync.dma_start(
+                out=tile[:, :, c0:c1].bitcast(I32),
+                in_=src[:, :, c0:c1].rearrange("g p n -> p g n").bitcast(I32),
+            )
+
+        load_scales(xt_s, xt_scales)
+        load_scales(a_s, a_scales)
+        load_words(xt_w, xt_words, 0, 1024)
+        for c0, c1 in ((0, 2), (2, 4), (4, 8)):
+            load_words(a_w, a_words, 256 * c0, 256 * c1)
+            load_words(a_w, a_words, 2 * N + 256 * c0, 2 * N + 256 * c1)
+        row = 0
+        for v in (gain1, shift1, gain2, shift2, skip):
+            rows = v.shape[0] // P
+            nc.scalar.dma_start(out=vec_in[row : row + rows, :], in_=v.rearrange("(c p) -> c p", p=P))
+            row += rows
+        load_words(xt_w, xt_words, 1024, 1536)
+        load_scales(b_s, b_scales)
+        load_words(b_w, b_words, 0, 4 * N)
+        nc.sync.dma_start(out=dp[:], in_=d_prev.rearrange("(v s) c -> s v c", s=V))
+
+        nc.vector.tensor_copy(out=vec_in32[:], in_=vec_in[:])
+        vec_ps = psum.tile([P, 512], F32, tag="tr", bufs=2, name="vec_ps")
+        nc.tensor.transpose(vec_ps[:, 0:P], vec_in32[:], ident[:])
+        nc.vector.tensor_copy(out=vec[:], in_=vec_ps[:, 0:P])
+        for c0, c1 in ((40, 48), (56, 72)):
+            nc.vector.tensor_scalar_mul(vec[:, c0:c1], vec[:, c0:c1], ROOT_HALF)
+
+        units = []
+        for stage in range(2):
+            units += [(stage, c, 1, 0, 512) for c in range(8)]
+            units += [(stage, c, 2, 512, 256) for c in range(0, 8, 2)]
+        n_units = len(units)
+        state = [dict() for u in units]
+        pre = {}
+
+        def mm(u):
+            stage, c, nt, s0, ns = units[u]
+            banks = []
+            for half in range(2):
+                bank = psum.tile([P, 512], F32, tag="mm", name="bank")
+                banks.append(bank)
+                for q in range(nt):
+                    col = half * N + P * (c + q)
+                    if stage == 0:
+                        for g in range(GK):
+                            nc.tensor.matmul_mx(
+                                out=bank[:, q * ns : (q + 1) * ns],
+                                lhsT=a_w[:, g, 2 * col : 2 * col + 2 * P].bitcast(FP4X4),
+                                lhsT_scale=a_s[:, g, col : col + P],
+                                rhs=xt_w[:, g, 2 * s0 : 2 * (s0 + ns)].bitcast(FP4X4),
+                                rhs_scale=xt_s[:, g, s0 : s0 + ns],
+                                start=(g == 0),
+                                stop=(g == GK - 1),
+                            )
+                    else:
+                        w = 512 if ns == 512 else 128
+                        for r in range(0, ns, w):
+                            for g in range(GN):
+                                nc.tensor.matmul_mx(
+                                    out=bank[:, q * ns + r : q * ns + r + w],
+                                    lhsT=b_w[:, g, 2 * col : 2 * col + 2 * P].bitcast(FP4X4),
+                                    lhsT_scale=b_s[:, g, col : col + P],
+                                    rhs=hc[:, g, s0 + r : s0 + r + w].bitcast(FP8X4),
+                                    rhs_scale=hs[:, g, s0 + r : s0 + r + w],
+                                    start=(g == 0),
+                                    stop=(g == GN - 1),
+                                )
+            state[u]["banks"] = banks
+
+        def stats(u):
+            st = work.tile([P, 4, 6], F32, name="st")
+            for half in range(2):
+                for q in range(2):
+                    nc.vector.bn_stats(
+                        out=st[:, 2 * half + q, :],
+                        in_=state[u]["banks"][half][:, 256 * q : 256 * q + 256].rearrange("p (e s) -> p s e", e=2),
+                    )
+            state[u]["st"] = st
+
+        def small(u):
+            stage, c, nt, s0, ns = units[u]
+            nv = ns // V
+            flat = state[u]["st"][:].rearrange("p k (e s) -> p (k e) s", e=2)
+            mean = flat[:, :, 1]
+            m2 = flat[:, :, 2]
+
+            def per_block(base):
+                cols = vec[:, base : base + 16].rearrange("p (h c o) -> p h c o", h=2, o=1)
+                return cols[:, :, c : c + nt, :].to_broadcast([P, 2, nt, nv])
+
+            shape = "p (h c v) -> p h c v"
+            var = work.tile([P, 8], F32, name="var")
+            nc.gpsimd.tensor_scalar(out=var[:], in0=m2, scalar1=1.0 / V, scalar2=EPS, op0=MULT, op1=ADD)
+            rstd = work.tile([P, 8], F32, name="rstd")
+            nc.gpsimd.tensor_tensor(out=rstd[:], in0=var[:], in1=neg_half[:], op=POW)
+            mul = work.tile([P, 8], F32, name="mul")
+            nc.gpsimd.tensor_tensor(
+                out=mul[:].rearrange(shape, h=2, c=nt),
+                in0=rstd[:].rearrange(shape, h=2, c=nt),
+                in1=per_block(32 * stage),
+                op=MULT,
+            )
+            mm_ = work.tile([P, 8], F32, name="mean_mul")
+            nc.gpsimd.tensor_tensor(out=mm_[:], in0=mean, in1=mul[:], op=MULT)
+            off = work.tile([P, 8], F32, name="off")
+            nc.gpsimd.tensor_tensor(
+                out=off[:].rearrange(shape, h=2, c=nt),
+                in0=per_block(32 * stage + 16),
+                in1=mm_[:].rearrange(shape, h=2, c=nt),
+                op=SUB,
+            )
+            state[u]["mul"] = mul
+            state[u]["off"] = off
+
+        def act(u):
+            mul, off = state[u]["mul"], state[u]["off"]
+            gate = work.tile([P, 512], F32, name="gate")
+            lin = work.tile([P, 512], F32, name="lin")
+            for half, dst, func in ((0, gate, SIGMOID), (1, lin, IDENTITY)):
+                for j in range(4):
+                    k = 4 * half + j
+                    nc.scalar.activation(
+                        out=dst[:, P * j : P * j + P],
+                        in_=state[u]["banks"][half][:, P * j : P * j + P],
+                        func=func,
+                        scale=mul[:, k : k + 1],
+                        bias=off[:, k : k + 1],
+                    )
+            state[u]["gate"], state[u]["lin"] = gate, lin
+
+        def h_view(u):
+            stage, c, nt, s0, ns = units[u]
+            return h_all[:, c : c + nt, s0 : s0 + ns]
+
+        def product(u):
+            stage, c, nt, s0, ns = units[u]
+            if stage == 0:
+                dst = h_view(u)
+            else:
+                prod = work.tile([P, 512], F32, name="prod")
+                state[u]["prod"] = prod
+                dst = prod[:].rearrange("p (c s) -> p c s", c=nt)
+            nc.vector.tensor_tensor(
+                out=dst,
+                in0=state[u]["gate"][:].rearrange("p (c s) -> p c s", c=nt),
+                in1=state[u]["lin"][:].rearrange("p (c s) -> p c s", c=nt),
+                op=MULT,
+            )
+
+        def spread(u):
+            stage, c, nt, s0, ns = units[u]
+            for q in range(nt):
+                g, r = divmod(c + q, 4)
+                if (s0, g) not in pre:
+                    pre[(s0, g)] = keep.tile([P, 4, ns], F32, name="pre%d_%d" % (s0, g))
+                for t in range(4):
+                    nc.sync.dma_start(
+                        out=pre[(s0, g)][32 * r : 32 * r + 32, t, :],
+                        in_=h_all[t:P:4, c + q, s0 : s0 + ns],
+                    )
+
+        def group(s0, ns, g):
+            grouped = work.tile([P, 512, 4], BF16, align_bytes=64, bufs=2, name="grouped")
+            nc.vector.tensor_copy(out=grouped[:, 0:ns, :], in_=pre[(s0, g)][:].rearrange("p t n -> p n t"))
+            state[0]["grouped"] = grouped
+
+        def quant(s0, ns, g):
+            nc.vector.quantize_mx(
+                out=hc[:, g, s0 : s0 + ns].bitcast(FP8X4),
+                scales=hs[:, g, s0 : s0 + ns],
+                in_=state[0]["grouped"][:, 0:ns, :].rearrange("p n t -> p (n t)"),
+            )
+
+        def final(u):
+            stage, c, nt, s0, ns = units[u]
+            y = work.tile([P, 512], F32, name="y")
+            for q in range(nt):
+                cols = slice(q * ns, (q + 1) * ns)
+                nc.vector.scalar_tensor_tensor(
+                    out=y[:, cols],
+                    in0=h_all[:, c + q, s0 : s0 + ns],
+                    scalar=vec[:, 64 + c + q : 65 + c + q],
+                    in1=state[u]["prod"][:, cols],
+                    op0=MULT,
+                    op1=ADD,
+                )
+            state[u]["y"] = y
+
+        def turn(u):
+            stage, c, nt, s0, ns = units[u]
+            nv = ns // V
+            bank = psum.tile([P, 512], F32, tag="tr", bufs=2, name="turned")
+            for v in range(nv):
+                for q in range(nt):
+                    nc.tensor.transpose(
+                        bank[:, P * (v * nt + q) : P * (v * nt + q) + P],
+                        state[u]["y"][:, q * ns + V * v : q * ns + V * v + V],
+                        ident[:],
+                    )
+            state[u]["turned"] = bank
+
+        def leave(u):
+            stage, c, nt, s0, ns = units[u]
+            nv, v0 = ns // V, s0 // V
+            turned = state[u]["turned"][:].rearrange("p (v c) -> p v c", v=nv)
+            res = work.tile([P, 512], F32, name="res")
+            res_v = res[:].rearrange("p (v c) -> p v c", v=nv)
+            col = P * c % D
+            if P * c < D:
+                nc.vector.scalar_tensor_tensor(
+                    out=res_v, in0=turned, scalar=0.0,
+                    in1=dp[:, v0 : v0 + nv, col : col + P * nt], op0=MAX, op1=ADD,
+                )
+                dst = out_0
+            else:
+                nc.scalar.copy(out=res_v, in_=turned)
+                dst = out_1
+            nc.sync.dma_start(
+                out=dst[s0 : s0 + ns, col : col + P * nt].rearrange("(v s) c -> s v c", s=V),
+                in_=res_v,
+            )
+
+        half_units = n_units // 2
+        mm(0)
+        mm(1)
+        stats(0)
+        small(0)
+        quants = {6: (0, 512, 0), 9: (0, 512, 1), 13: (512, 256, 0), 14: (512, 256, 1)}
+        for i in range(n_units + 2):
+            if i in quants:
+                group(*quants[i])
+            if i + 1 < n_units:
+                stats(i + 1)
+                small(i + 1)
+            if i in quants:
+                quant(*quants[i])
+            if i + 2 < n_units:
+                mm(i + 2)
+            if i < n_units:
+                act(i)
+            if half_units <= i - 1 < n_units:
+                final(i - 1)
+                turn(i - 1)
+            if half_units <= i - 2 < n_units:
+                leave(i - 2)
+            if i < n_units:
+                product(i)
+                if i < half_units:
+                    spread(i)

@@ -20,13 +20,25 @@ ADD = mybir.AluOpType.add
 MULT = mybir.AluOpType.mult
 SUB = mybir.AluOpType.subtract
 MAX = mybir.AluOpType.max
-POW = mybir.AluOpType.pow
+SHR = mybir.AluOpType.logical_shift_right
+XOR = mybir.AluOpType.bitwise_xor
 SIGMOID = mybir.ActivationFunctionType.Sigmoid
 IDENTITY = mybir.ActivationFunctionType.Identity
+SQUARE = mybir.ActivationFunctionType.Square
+
+K1 = 2.0**124.87
+K2 = K1 * (3.0 / 8.0) ** 2
+K3 = K1**0.5 * (3.0 / 8.0) ** 2
 
 P = 128
 GK = K // 512
 GN = N // 512
+C = 256
+CHUNKS = M // C
+STEPS = 2 * CHUNKS * 2
+ACT_GROUPS = True
+EARLY = 3
+RATE = 2
 
 
 def tile_tabnet_glu_step_f2_kernel(
@@ -37,7 +49,7 @@ def tile_tabnet_glu_step_f2_kernel(
     with ExitStack() as ctx:
         keep = ctx.enter_context(tc.tile_pool(name="keep", bufs=1))
         work = ctx.enter_context(tc.tile_pool(name="work", bufs=3))
-        psum = ctx.enter_context(tc.psum_pool(name="psum", bufs=6))
+        psum = ctx.enter_context(tc.psum_pool(name="psum", bufs=7))
         ctx.enter_context(tc.manual_schedule())
 
         xt_w = keep.tile([P, GK, 2 * M], U8, align_bytes=64, name="xt_w")
@@ -50,19 +62,19 @@ def tile_tabnet_glu_step_f2_kernel(
         vec_in32 = keep.tile([P, P], F32, name="vec_in32")
         vec = keep.tile([P, P], F32, name="vec")
         ident = keep.tile([P, P], F32, name="ident")
-        neg_half = keep.tile([P, 8], F32, name="neg_half")
+        gain = keep.tile([P, 64], F32, name="gain")
+        shift = keep.tile([P, 64], F32, name="shift")
         warm = keep.tile([P, 1], F32, name="warm")
         dp = keep.tile([P, M // V, D], BF16, name="dp")
         h_all = keep.tile([P, N // P, M], F32, name="h_all")
         hc = keep.tile([P, GN, M], U32, align_bytes=64, name="hc")
         hs = keep.tile([P, GN, M], U8, align_bytes=64, name="hs")
 
+        nc.vector.memset(vec_in[:], 0.0)
         nc.vector.memset(xt_s[:].rearrange("p g n -> p (g n)").bitcast(I32), 0)
         nc.vector.memset(a_s[:].rearrange("p g n -> p (g n)").bitcast(I32), 0)
-        nc.vector.memset(vec_in[:], 0.0)
         nc.vector.memset(b_s[:].rearrange("p g n -> p (g n)").bitcast(I32), 0)
         nc.gpsimd.memset(warm[:], 0.0)
-        nc.gpsimd.memset(neg_half[:], -0.5)
         make_identity(nc, ident[:])
         nc.scalar.activation(out=warm[:], in_=warm[:], func=SIGMOID)
 
@@ -79,183 +91,211 @@ def tile_tabnet_glu_step_f2_kernel(
                 in_=src[:, :, c0:c1].rearrange("g p n -> p g n").bitcast(I32),
             )
 
-        load_scales(xt_s, xt_scales)
-        load_scales(a_s, a_scales)
-        load_words(xt_w, xt_words, 0, 1024)
-        for c0, c1 in ((0, 2), (2, 4), (4, 8)):
-            load_words(a_w, a_words, 256 * c0, 256 * c1)
-            load_words(a_w, a_words, 2 * N + 256 * c0, 2 * N + 256 * c1)
         row = 0
         for v in (gain1, shift1, gain2, shift2, skip):
             rows = v.shape[0] // P
             nc.scalar.dma_start(out=vec_in[row : row + rows, :], in_=v.rearrange("(c p) -> c p", p=P))
             row += rows
-        load_words(xt_w, xt_words, 1024, 1536)
+        load_scales(xt_s, xt_scales)
+        load_scales(a_s, a_scales)
+        load_words(xt_w, xt_words, 0, 512)
+        for c0, c1 in ((0, 2), (2, 4), (4, 8)):
+            load_words(a_w, a_words, 256 * c0, 256 * c1)
+            load_words(a_w, a_words, 2 * N + 256 * c0, 2 * N + 256 * c1)
+        load_words(xt_w, xt_words, 512, 1536)
         load_scales(b_s, b_scales)
         load_words(b_w, b_words, 0, 4 * N)
         nc.sync.dma_start(out=dp[:], in_=d_prev.rearrange("(v s) c -> s v c", s=V))
 
-        nc.vector.tensor_copy(out=vec_in32[:], in_=vec_in[:])
-        vec_ps = psum.tile([P, 512], F32, tag="tr", bufs=2, name="vec_ps")
-        nc.tensor.transpose(vec_ps[:, 0:P], vec_in32[:], ident[:])
-        nc.vector.tensor_copy(out=vec[:], in_=vec_ps[:, 0:P])
-        for c0, c1 in ((40, 48), (56, 72)):
-            nc.vector.tensor_scalar_mul(vec[:, c0:c1], vec[:, c0:c1], ROOT_HALF)
+        vec_ps = psum.tile([P, 512], F32, tag="tr", bufs=1, name="vec_ps")
 
-        units = []
-        for stage in range(2):
-            units += [(stage, c, 1, 0, 512) for c in range(8)]
-            units += [(stage, c, 2, 512, 256) for c in range(0, 8, 2)]
-        n_units = len(units)
-        state = [dict() for u in units]
-        pre = {}
+        def load_vectors(part):
+            if part == 0:
+                nc.vector.tensor_copy(out=vec_in32[:], in_=vec_in[:])
+                nc.tensor.transpose(vec_ps[:, 0:P], vec_in32[:], ident[:])
+                return
+            nc.vector.tensor_copy(out=vec[:], in_=vec_ps[:, 0:P])
+            for stage in range(2):
+                for dst, base, factor in ((gain, 32 * stage, K3), (shift, 32 * stage + 16, 1.0)):
+                    for half in range(2):
+                        f = factor * (ROOT_HALF if stage and half else 1.0)
+                        cols = vec[:, base + 8 * half : base + 8 * half + 8]
+                        spread_to = dst[:, 32 * stage : 32 * stage + 32]
+                        spread_to = spread_to.rearrange("p (u h c v) -> p h u c v", u=4, h=2, c=2)
+                        nc.gpsimd.tensor_scalar(
+                            out=spread_to[:, half, :, :, :],
+                            in0=cols.rearrange("p (u c o) -> p u c o", u=4, o=1).to_broadcast([P, 4, 2, 2]),
+                            scalar1=f, scalar2=0.0, op0=MULT, op1=ADD,
+                        )
+            nc.gpsimd.tensor_scalar(
+                out=vec[:, 64:72], in0=vec[:, 64:72], scalar1=ROOT_HALF, scalar2=0.0, op0=MULT, op1=ADD
+            )
+
+        def where(u):
+            b, half = divmod(u, 2)
+            stage, rest = divmod(b, 2 * CHUNKS)
+            chunk, g = divmod(rest, 2)
+            return stage, C * chunk, g, 4 * g + 2 * half
+
+        state = [dict() for u in range(2 * STEPS)]
+        pairs = [dict() for b in range(STEPS)]
 
         def mm(u):
-            stage, c, nt, s0, ns = units[u]
+            stage, s0, g_, c = where(u)
             banks = []
             for half in range(2):
-                bank = psum.tile([P, 512], F32, tag="mm", name="bank")
+                if u < STEPS and u % 4 == 3 and half == 1:
+                    bank = psum.tile([P, 512], F32, tag="tr", bufs=1, name="bank")
+                else:
+                    bank = psum.tile([P, 512], F32, tag="mm", name="bank")
                 banks.append(bank)
-                for q in range(nt):
+                for q in range(2):
                     col = half * N + P * (c + q)
-                    if stage == 0:
-                        for g in range(GK):
-                            nc.tensor.matmul_mx(
-                                out=bank[:, q * ns : (q + 1) * ns],
-                                lhsT=a_w[:, g, 2 * col : 2 * col + 2 * P].bitcast(FP4X4),
-                                lhsT_scale=a_s[:, g, col : col + P],
-                                rhs=xt_w[:, g, 2 * s0 : 2 * (s0 + ns)].bitcast(FP4X4),
-                                rhs_scale=xt_s[:, g, s0 : s0 + ns],
-                                start=(g == 0),
-                                stop=(g == GK - 1),
+                    words, scales, mov, mov_s, passes, width = (
+                        (a_w, a_s, xt_w, xt_s, GK, 256) if stage == 0 else (b_w, b_s, hc, hs, GN, 128)
+                    )
+                    for r in range(0, C, width):
+                        m0 = s0 + r
+                        for g in range(passes):
+                            rhs = (
+                                mov[:, g, 2 * m0 : 2 * (m0 + width)].bitcast(FP4X4)
+                                if stage == 0
+                                else mov[:, g, m0 : m0 + width].bitcast(FP8X4)
                             )
-                    else:
-                        w = 512 if ns == 512 else 128
-                        for r in range(0, ns, w):
-                            for g in range(GN):
-                                nc.tensor.matmul_mx(
-                                    out=bank[:, q * ns + r : q * ns + r + w],
-                                    lhsT=b_w[:, g, 2 * col : 2 * col + 2 * P].bitcast(FP4X4),
-                                    lhsT_scale=b_s[:, g, col : col + P],
-                                    rhs=hc[:, g, s0 + r : s0 + r + w].bitcast(FP8X4),
-                                    rhs_scale=hs[:, g, s0 + r : s0 + r + w],
-                                    start=(g == 0),
-                                    stop=(g == GN - 1),
-                                )
+                            nc.tensor.matmul_mx(
+                                out=bank[:, q * C + r : q * C + r + width],
+                                lhsT=words[:, g, 2 * col : 2 * col + 2 * P].bitcast(FP4X4),
+                                lhsT_scale=scales[:, g, col : col + P],
+                                rhs=rhs,
+                                rhs_scale=mov_s[:, g, m0 : m0 + width],
+                                start=(g == 0),
+                                stop=(g == passes - 1),
+                            )
             state[u]["banks"] = banks
 
-        def stats(u):
-            st = work.tile([P, 4, 6], F32, name="st")
-            for half in range(2):
-                for q in range(2):
-                    nc.vector.bn_stats(
-                        out=st[:, 2 * half + q, :],
-                        in_=state[u]["banks"][half][:, 256 * q : 256 * q + 256].rearrange("p (e s) -> p s e", e=2),
-                    )
-            state[u]["st"] = st
-
-        def small(u):
-            stage, c, nt, s0, ns = units[u]
-            nv = ns // V
-            flat = state[u]["st"][:].rearrange("p k (e s) -> p (k e) s", e=2)
-            mean = flat[:, :, 1]
-            m2 = flat[:, :, 2]
-
-            def per_block(base):
-                cols = vec[:, base : base + 16].rearrange("p (h c o) -> p h c o", h=2, o=1)
-                return cols[:, :, c : c + nt, :].to_broadcast([P, 2, nt, nv])
-
-            shape = "p (h c v) -> p h c v"
-            var = work.tile([P, 8], F32, name="var")
-            nc.gpsimd.tensor_scalar(out=var[:], in0=m2, scalar1=1.0 / V, scalar2=EPS, op0=MULT, op1=ADD)
-            rstd = work.tile([P, 8], F32, name="rstd")
-            nc.gpsimd.tensor_tensor(out=rstd[:], in0=var[:], in1=neg_half[:], op=POW)
-            mul = work.tile([P, 8], F32, name="mul")
-            nc.gpsimd.tensor_tensor(
-                out=mul[:].rearrange(shape, h=2, c=nt),
-                in0=rstd[:].rearrange(shape, h=2, c=nt),
-                in1=per_block(32 * stage),
-                op=MULT,
+        def stats(u, part):
+            pair = pairs[u // 2]
+            if u % 2 == 0 and part == 0:
+                pair["st"] = work.tile([P, 8, 6], F32, name="st")
+            half, q = divmod(part, 2)
+            nc.vector.bn_stats(
+                out=pair["st"][:, 4 * (u % 2) + part, :],
+                in_=state[u]["banks"][half][:, C * q : C * q + C].rearrange("p (e s) -> p s e", e=2),
             )
-            mm_ = work.tile([P, 8], F32, name="mean_mul")
-            nc.gpsimd.tensor_tensor(out=mm_[:], in0=mean, in1=mul[:], op=MULT)
-            off = work.tile([P, 8], F32, name="off")
-            nc.gpsimd.tensor_tensor(
-                out=off[:].rearrange(shape, h=2, c=nt),
-                in0=per_block(32 * stage + 16),
-                in1=mm_[:].rearrange(shape, h=2, c=nt),
-                op=SUB,
-            )
-            state[u]["mul"] = mul
-            state[u]["off"] = off
+
+        def chain(b):
+            pair = pairs[b]
+            flat = pair["st"][:].rearrange("p k (e s) -> p (k e) s", e=2)
+            mean, m2 = flat[:, :, 1], flat[:, :, 2]
+
+            def tile(name):
+                pair[name] = work.tile([P, 16], F32, name="chain_" + name)
+                return pair[name][:]
+
+            def square(out, in_, scale, bias):
+                nc.scalar.activation(out=tile(out), in_=pair[in_][:], func=SQUARE, scale=scale, bias=bias)
+
+            def times(out, in0, in1):
+                nc.vector.tensor_tensor(out=tile(out), in0=in0, in1=in1, op=MULT)
+
+            def step(out, in0, in1):
+                nc.vector.scalar_tensor_tensor(
+                    out=tile(out), in0=pair[in0][:], scalar=20.0 / 9.0, in1=pair[in1][:], op0=ADD, op1=MULT
+                )
+
+            cols = slice(16 * (2 * (b // (2 * CHUNKS)) + b % 2), 16 * (2 * (b // (2 * CHUNKS)) + b % 2) + 16)
+            on_act = [
+                lambda: nc.scalar.activation(out=tile("v"), in_=m2, func=IDENTITY, scale=1.0 / V, bias=EPS),
+                lambda: square("p1", "y0", K1**0.5, 0.0),
+                lambda: square("s1", "w1", 1.0, -5.0 / 3.0),
+                lambda: square("p2", "y1", K2**0.5, 0.0),
+                lambda: square("s2", "w2", 1.0, -5.0 / 3.0),
+            ]
+            on_dve = [
+                lambda: nc.vector.tensor_scalar(
+                    out=tile("y0").bitcast(I32), in0=pair["v"][:].bitcast(I32),
+                    scalar1=1, scalar2=0x3FFFFFFF, op0=SHR, op1=XOR,
+                ),
+                lambda: times("w1", pair["p1"][:], pair["v"][:]),
+                lambda: step("y1", "s1", "y0"),
+                lambda: times("w2", pair["p2"][:], pair["v"][:]),
+                lambda: step("y2", "s2", "y1"),
+                lambda: times("mul", pair["y2"][:], gain[:, cols]),
+                lambda: times("moved", mean, pair["mul"][:]),
+                lambda: nc.vector.tensor_tensor(out=tile("off"), in0=shift[:, cols], in1=pair["moved"][:], op=SUB),
+            ]
+            return on_act, on_dve
 
         def act(u):
-            mul, off = state[u]["mul"], state[u]["off"]
+            mul, off = pairs[u // 2]["mul"], pairs[u // 2]["off"]
             gate = work.tile([P, 512], F32, name="gate")
             lin = work.tile([P, 512], F32, name="lin")
-            for half, dst, func in ((0, gate, SIGMOID), (1, lin, IDENTITY)):
-                for j in range(4):
-                    k = 4 * half + j
-                    nc.scalar.activation(
-                        out=dst[:, P * j : P * j + P],
-                        in_=state[u]["banks"][half][:, P * j : P * j + P],
-                        func=func,
-                        scale=mul[:, k : k + 1],
-                        bias=off[:, k : k + 1],
-                    )
             state[u]["gate"], state[u]["lin"] = gate, lin
 
-        def h_view(u):
-            stage, c, nt, s0, ns = units[u]
-            return h_all[:, c : c + nt, s0 : s0 + ns]
+            def block(half, j):
+                k = 8 * (u % 2) + 4 * half + j
+                nc.scalar.activation(
+                    out=(gate, lin)[half][:, P * j : P * j + P],
+                    in_=state[u]["banks"][half][:, P * j : P * j + P],
+                    func=(SIGMOID, IDENTITY)[half],
+                    scale=mul[:, k : k + 1],
+                    bias=off[:, k : k + 1],
+                )
+
+            return [lambda half=half, j=j: block(half, j) for half in range(2) for j in range(4)]
 
         def product(u):
-            stage, c, nt, s0, ns = units[u]
+            stage, s0, g, c = where(u)
             if stage == 0:
-                dst = h_view(u)
+                dst = h_all[:, c : c + 2, s0 : s0 + C]
             else:
                 prod = work.tile([P, 512], F32, name="prod")
                 state[u]["prod"] = prod
-                dst = prod[:].rearrange("p (c s) -> p c s", c=nt)
+                dst = prod[:].rearrange("p (c s) -> p c s", c=2)
             nc.vector.tensor_tensor(
                 out=dst,
-                in0=state[u]["gate"][:].rearrange("p (c s) -> p c s", c=nt),
-                in1=state[u]["lin"][:].rearrange("p (c s) -> p c s", c=nt),
+                in0=state[u]["gate"][:].rearrange("p (c s) -> p c s", c=2),
+                in1=state[u]["lin"][:].rearrange("p (c s) -> p c s", c=2),
                 op=MULT,
             )
 
         def spread(u):
-            stage, c, nt, s0, ns = units[u]
-            for q in range(nt):
-                g, r = divmod(c + q, 4)
-                if (s0, g) not in pre:
-                    pre[(s0, g)] = keep.tile([P, 4, ns], F32, name="pre%d_%d" % (s0, g))
+            stage, s0, g, c = where(u)
+            if u % 2 == 0:
+                pairs[u // 2]["pre"] = work.tile([P, 4, C], F32, name="pre")
+            for q in range(2):
+                r = (c + q) % 4
                 for t in range(4):
                     nc.sync.dma_start(
-                        out=pre[(s0, g)][32 * r : 32 * r + 32, t, :],
-                        in_=h_all[t:P:4, c + q, s0 : s0 + ns],
+                        out=pairs[u // 2]["pre"][32 * r : 32 * r + 32, t, :],
+                        in_=h_all[t:P:4, c + q, s0 : s0 + C],
                     )
 
-        def group(s0, ns, g):
-            grouped = work.tile([P, 512, 4], BF16, align_bytes=64, bufs=2, name="grouped")
-            nc.vector.tensor_copy(out=grouped[:, 0:ns, :], in_=pre[(s0, g)][:].rearrange("p t n -> p n t"))
-            state[0]["grouped"] = grouped
+        def group(b):
+            grouped = work.tile([P, C, 4], BF16, align_bytes=64, name="grouped")
+            pairs[b]["grouped"] = grouped
+            src = pairs[b]["pre"][:].rearrange("p t n -> p n t")
+            if ACT_GROUPS:
+                nc.scalar.copy(out=grouped[:], in_=src)
+            else:
+                nc.vector.tensor_copy(out=grouped[:], in_=src)
 
-        def quant(s0, ns, g):
+        def quant(b):
+            stage, s0, g, c = where(2 * b)
             nc.vector.quantize_mx(
-                out=hc[:, g, s0 : s0 + ns].bitcast(FP8X4),
-                scales=hs[:, g, s0 : s0 + ns],
-                in_=state[0]["grouped"][:, 0:ns, :].rearrange("p n t -> p (n t)"),
+                out=hc[:, g, s0 : s0 + C].bitcast(FP8X4),
+                scales=hs[:, g, s0 : s0 + C],
+                in_=pairs[b]["grouped"][:].rearrange("p n t -> p (n t)"),
             )
 
         def final(u):
-            stage, c, nt, s0, ns = units[u]
+            stage, s0, g, c = where(u)
             y = work.tile([P, 512], F32, name="y")
-            for q in range(nt):
-                cols = slice(q * ns, (q + 1) * ns)
+            for q in range(2):
+                cols = slice(q * C, (q + 1) * C)
                 nc.vector.scalar_tensor_tensor(
                     out=y[:, cols],
-                    in0=h_all[:, c + q, s0 : s0 + ns],
+                    in0=h_all[:, c + q, s0 : s0 + C],
                     scalar=vec[:, 64 + c + q : 65 + c + q],
                     in1=state[u]["prod"][:, cols],
                     op0=MULT,
@@ -264,63 +304,117 @@ def tile_tabnet_glu_step_f2_kernel(
             state[u]["y"] = y
 
         def turn(u):
-            stage, c, nt, s0, ns = units[u]
-            nv = ns // V
-            bank = psum.tile([P, 512], F32, tag="tr", bufs=2, name="turned")
-            for v in range(nv):
-                for q in range(nt):
+            bank = psum.tile([P, 512], F32, tag="tr", bufs=1, name="turned")
+            for v in range(2):
+                for q in range(2):
                     nc.tensor.transpose(
-                        bank[:, P * (v * nt + q) : P * (v * nt + q) + P],
-                        state[u]["y"][:, q * ns + V * v : q * ns + V * v + V],
+                        bank[:, P * (2 * v + q) : P * (2 * v + q) + P],
+                        state[u]["y"][:, q * C + V * v : q * C + V * v + V],
                         ident[:],
                     )
             state[u]["turned"] = bank
 
         def leave(u):
-            stage, c, nt, s0, ns = units[u]
-            nv, v0 = ns // V, s0 // V
-            turned = state[u]["turned"][:].rearrange("p (v c) -> p v c", v=nv)
+            stage, s0, g, c = where(u)
+            v0 = s0 // V
+            turned = state[u]["turned"][:].rearrange("p (v c) -> p v c", v=2)
             res = work.tile([P, 512], F32, name="res")
-            res_v = res[:].rearrange("p (v c) -> p v c", v=nv)
+            res_v = res[:].rearrange("p (v c) -> p v c", v=2)
             col = P * c % D
-            if P * c < D:
+            if g == 0:
                 nc.vector.scalar_tensor_tensor(
                     out=res_v, in0=turned, scalar=0.0,
-                    in1=dp[:, v0 : v0 + nv, col : col + P * nt], op0=MAX, op1=ADD,
+                    in1=dp[:, v0 : v0 + 2, col : col + 2 * P], op0=MAX, op1=ADD,
                 )
-                dst = out_0
             else:
                 nc.scalar.copy(out=res_v, in_=turned)
-                dst = out_1
             nc.sync.dma_start(
-                out=dst[s0 : s0 + ns, col : col + P * nt].rearrange("(v s) c -> s v c", s=V),
+                out=(out_0, out_1)[g][s0 : s0 + C, col : col + 2 * P].rearrange("(v s) c -> s v c", s=V),
                 in_=res_v,
             )
 
-        half_units = n_units // 2
+        urgent = []
+        waiting = []
+        emitted = set()
+
+        def emit(queue, count):
+            for i in range(min(count, len(queue))):
+                queue.pop(0)()
+
+        def emit_act(count):
+            for i in range(count):
+                emit(urgent if urgent else waiting, 1)
+
+        def need(key):
+            while key not in emitted:
+                emit_act(1)
+
+        def mark(key, work_item):
+            work_item()
+            emitted.add(key)
+
+        def quant_when_grouped(b):
+            need(("group", b))
+            quant(b)
+
+        def finish(u):
+            final(u)
+            turn(u)
+            if where(u)[2] == 1:
+                urgent.append(lambda: leave(u))
+
+        def multiply(u):
+            need(("act", u))
+            product(u)
+            if u < STEPS:
+                spread(u)
+
         mm(0)
         mm(1)
-        stats(0)
-        small(0)
-        quants = {6: (0, 512, 0), 9: (0, 512, 1), 13: (512, 256, 0), 14: (512, 256, 1)}
-        for i in range(n_units + 2):
-            if i in quants:
-                group(*quants[i])
-            if i + 1 < n_units:
-                stats(i + 1)
-                small(i + 1)
-            if i in quants:
-                quant(*quants[i])
-            if i + 2 < n_units:
-                mm(i + 2)
-            if i < n_units:
-                act(i)
-            if half_units <= i - 1 < n_units:
-                final(i - 1)
-                turn(i - 1)
-            if half_units <= i - 2 < n_units:
-                leave(i - 2)
-            if i < n_units:
-                product(i)
-                if i < half_units:
-                    spread(i)
+        load_vectors(0)
+        for part in range(8):
+            stats(part // 4, part % 4)
+        load_vectors(1)
+        mm(2)
+        mm(3)
+        for b in range(STEPS + 3):
+            dve = []
+            ahead = []
+            if b + 1 < STEPS:
+                for part in range(8):
+                    ahead.append(lambda u=2 * b + 2 + part // 4, part=part % 4: stats(u, part))
+            for half in range(2):
+                end, new, old = 2 * b - 4 + half, 2 * b + 2 + half, 2 * b - 2 + half
+                ending = STEPS <= end < 2 * STEPS
+                if ending:
+                    dve.append(lambda u=end: finish(u))
+                if 4 <= new < 2 * STEPS:
+                    dve.append(lambda u=new: mm(u))
+                if 0 <= old < 2 * STEPS:
+                    if not ending:
+                        dve += ahead[:EARLY]
+                        ahead = ahead[EARLY:]
+                    dve.append(lambda u=old: multiply(u))
+                if ending and where(end)[2] == 0:
+                    dve.append(lambda u=end: leave(u))
+            if 0 <= b - 3 < STEPS // 2:
+                waiting.append(lambda b=b: mark(("group", b - 3), lambda: group(b - 3)))
+                dve.append(lambda b=b: quant_when_grouped(b - 3))
+            dve += ahead
+            if b < STEPS:
+                on_act, on_dve = chain(b)
+                for r in range(8):
+                    emit(on_act, 1)
+                    emit_act(2)
+                    emit(dve, 1)
+                    on_dve[r]()
+                for u in (2 * b, 2 * b + 1):
+                    blocks = act(u)
+                    waiting += blocks[:-1]
+                    waiting.append(lambda u=u, last=blocks[-1]: mark(("act", u), last))
+                while dve:
+                    emit(dve, 1)
+                    emit_act(RATE)
+            else:
+                emit(dve, 99)
+                emit_act(99)

@@ -37,8 +37,10 @@ C = 256
 CHUNKS = M // C
 STEPS = 2 * CHUNKS * 2
 ACT_GROUPS = True
-EARLY = 3
-RATE = 2
+AFF_S1 = 1
+AFF_EVEN = 4
+AFF_ODD = 0
+PL1 = 3
 
 
 def tile_tabnet_glu_step_f2_kernel(
@@ -49,7 +51,7 @@ def tile_tabnet_glu_step_f2_kernel(
     with ExitStack() as ctx:
         keep = ctx.enter_context(tc.tile_pool(name="keep", bufs=1))
         work = ctx.enter_context(tc.tile_pool(name="work", bufs=3))
-        psum = ctx.enter_context(tc.psum_pool(name="psum", bufs=7))
+        psum = ctx.enter_context(tc.psum_pool(name="psum", bufs=6))
         ctx.enter_context(tc.manual_schedule())
 
         xt_w = keep.tile([P, GK, 2 * M], U8, align_bytes=64, name="xt_w")
@@ -59,23 +61,22 @@ def tile_tabnet_glu_step_f2_kernel(
         b_w = keep.tile([P, GN, 4 * N], U8, align_bytes=64, name="b_w")
         b_s = keep.tile([P, GN, 2 * N], U8, align_bytes=64, name="b_s")
         vec_in = keep.tile([P, P], BF16, name="vec_in")
-        vec_in32 = keep.tile([P, P], F32, name="vec_in32")
+        ident_bf = keep.tile([P, P], BF16, name="ident_bf")
         vec = keep.tile([P, P], F32, name="vec")
         ident = keep.tile([P, P], F32, name="ident")
         gain = keep.tile([P, 64], F32, name="gain")
         shift = keep.tile([P, 64], F32, name="shift")
         warm = keep.tile([P, 1], F32, name="warm")
         dp = keep.tile([P, M // V, D], BF16, name="dp")
-        h_all = keep.tile([P, N // P, M], F32, name="h_all")
+        hs_all = keep.tile([P, N // P, M], F32, name="hs_all")
         hc = keep.tile([P, GN, M], U32, align_bytes=64, name="hc")
         hs = keep.tile([P, GN, M], U8, align_bytes=64, name="hs")
 
-        nc.vector.memset(vec_in[:], 0.0)
+        nc.vector.memset(warm[:], 0.0)
         nc.vector.memset(xt_s[:].rearrange("p g n -> p (g n)").bitcast(I32), 0)
         nc.vector.memset(a_s[:].rearrange("p g n -> p (g n)").bitcast(I32), 0)
+        nc.vector.memset(vec_in[:], 0.0)
         nc.vector.memset(b_s[:].rearrange("p g n -> p (g n)").bitcast(I32), 0)
-        nc.gpsimd.memset(warm[:], 0.0)
-        make_identity(nc, ident[:])
         nc.scalar.activation(out=warm[:], in_=warm[:], func=SIGMOID)
 
         def load_scales(plane, src):
@@ -85,34 +86,37 @@ def tile_tabnet_glu_step_f2_kernel(
                     in_=src[:, 4 * q : 4 * q + 4, :].rearrange("g q n -> q g n").bitcast(I32),
                 )
 
-        def load_words(tile, src, c0, c1):
-            nc.sync.dma_start(
+        def load_words(tile, src, c0, c1, queue=nc.sync):
+            queue.dma_start(
                 out=tile[:, :, c0:c1].bitcast(I32),
                 in_=src[:, :, c0:c1].rearrange("g p n -> p g n").bitcast(I32),
             )
 
+        load_words(xt_w, xt_words, 0, 512, nc.gpsimd)
+        load_words(a_w, a_words, 2 * N, 2 * N + 512, nc.gpsimd)
+        load_words(a_w, a_words, 0, 512, nc.gpsimd)
+        make_identity(nc, ident[:])
         row = 0
         for v in (gain1, shift1, gain2, shift2, skip):
             rows = v.shape[0] // P
-            nc.scalar.dma_start(out=vec_in[row : row + rows, :], in_=v.rearrange("(c p) -> c p", p=P))
+            nc.gpsimd.dma_start(out=vec_in[row : row + rows, :], in_=v.rearrange("(c p) -> c p", p=P))
             row += rows
         load_scales(xt_s, xt_scales)
         load_scales(a_s, a_scales)
-        load_words(xt_w, xt_words, 0, 512)
-        for c0, c1 in ((0, 2), (2, 4), (4, 8)):
-            load_words(a_w, a_words, 256 * c0, 256 * c1)
+        for c0, c1 in ((2, 4), (4, 8)):
             load_words(a_w, a_words, 2 * N + 256 * c0, 2 * N + 256 * c1)
+            load_words(a_w, a_words, 256 * c0, 256 * c1)
         load_words(xt_w, xt_words, 512, 1536)
         load_scales(b_s, b_scales)
         load_words(b_w, b_words, 0, 4 * N)
         nc.sync.dma_start(out=dp[:], in_=d_prev.rearrange("(v s) c -> s v c", s=V))
 
-        vec_ps = psum.tile([P, 512], F32, tag="tr", bufs=1, name="vec_ps")
+        nc.vector.tensor_copy(out=ident_bf[:], in_=ident[:])
+        vec_ps = psum.tile([P, 1024], BF16, tag="gate", name="vec_ps")
 
         def load_vectors(part):
             if part == 0:
-                nc.vector.tensor_copy(out=vec_in32[:], in_=vec_in[:])
-                nc.tensor.transpose(vec_ps[:, 0:P], vec_in32[:], ident[:])
+                nc.tensor.transpose(vec_ps[:, 0:P], vec_in[:], ident_bf[:])
                 return
             nc.vector.tensor_copy(out=vec[:], in_=vec_ps[:, 0:P])
             for stage in range(2):
@@ -140,50 +144,53 @@ def tile_tabnet_glu_step_f2_kernel(
         state = [dict() for u in range(2 * STEPS)]
         pairs = [dict() for b in range(STEPS)]
 
-        def mm(u):
+        def mm(u, half):
             stage, s0, g_, c = where(u)
-            banks = []
-            for half in range(2):
-                if u < STEPS and u % 4 == 3 and half == 1:
-                    bank = psum.tile([P, 512], F32, tag="tr", bufs=1, name="bank")
-                else:
-                    bank = psum.tile([P, 512], F32, tag="mm", name="bank")
-                banks.append(bank)
-                for q in range(2):
-                    col = half * N + P * (c + q)
-                    words, scales, mov, mov_s, passes, width = (
-                        (a_w, a_s, xt_w, xt_s, GK, 256) if stage == 0 else (b_w, b_s, hc, hs, GN, 128)
-                    )
-                    for r in range(0, C, width):
-                        m0 = s0 + r
-                        for g in range(passes):
-                            rhs = (
-                                mov[:, g, 2 * m0 : 2 * (m0 + width)].bitcast(FP4X4)
-                                if stage == 0
-                                else mov[:, g, m0 : m0 + width].bitcast(FP8X4)
-                            )
-                            nc.tensor.matmul_mx(
-                                out=bank[:, q * C + r : q * C + r + width],
-                                lhsT=words[:, g, 2 * col : 2 * col + 2 * P].bitcast(FP4X4),
-                                lhsT_scale=scales[:, g, col : col + P],
-                                rhs=rhs,
-                                rhs_scale=mov_s[:, g, m0 : m0 + width],
-                                start=(g == 0),
-                                stop=(g == passes - 1),
-                            )
-            state[u]["banks"] = banks
-
-        def stats(u, part):
-            pair = pairs[u // 2]
-            if u % 2 == 0 and part == 0:
-                pair["st"] = work.tile([P, 8, 6], F32, name="st")
-            half, q = divmod(part, 2)
-            nc.vector.bn_stats(
-                out=pair["st"][:, 4 * (u % 2) + part, :],
-                in_=state[u]["banks"][half][:, C * q : C * q + C].rearrange("p (e s) -> p s e", e=2),
+            if half == 0:
+                bank = psum.tile([P, 512], F32, tag="gate", name="bank")
+            elif stage == 0 and u % 2:
+                bank = psum.tile([P, 512], F32, tag="turned", bufs=1, name="bank")
+            else:
+                bank = psum.tile([P, 512], F32, tag="linear", bufs=1, name="bank")
+            state[u][half] = bank
+            words, scales, mov, mov_s, passes, width = (
+                (a_w, a_s, xt_w, xt_s, GK, 256) if stage == 0 else (b_w, b_s, hc, hs, GN, 128)
             )
+            for q in range(2):
+                col = half * N + P * (c + q)
+                for r in range(0, C, width):
+                    m0 = s0 + r
+                    for g in range(passes):
+                        rhs = (
+                            mov[:, g, 2 * m0 : 2 * (m0 + width)].bitcast(FP4X4)
+                            if stage == 0
+                            else mov[:, g, m0 : m0 + width].bitcast(FP8X4)
+                        )
+                        nc.tensor.matmul_mx(
+                            out=bank[:, q * C + r : q * C + r + width],
+                            lhsT=words[:, g, 2 * col : 2 * col + 2 * P].bitcast(FP4X4),
+                            lhsT_scale=scales[:, g, col : col + P],
+                            rhs=rhs,
+                            rhs_scale=mov_s[:, g, m0 : m0 + width],
+                            start=(g == 0),
+                            stop=(g == passes - 1),
+                        )
 
-        def chain(b):
+        def take(u):
+            state[u]["raw"] = work.tile([P, 512], F32, bufs=7, name="raw")
+            nc.scalar.copy(out=state[u]["raw"][:], in_=state[u][1][:])
+
+        def stats(u, half):
+            pair = pairs[u // 2]
+            if "st" not in pair:
+                pair["st"] = work.tile([P, 8, 6], F32, name="st")
+            for q in range(2):
+                nc.vector.bn_stats(
+                    out=pair["st"][:, 4 * (u % 2) + 2 * half + q, :],
+                    in_=state[u][half][:, C * q : C * q + C].rearrange("p (e s) -> p s e", e=2),
+                )
+
+        def chain(b, both=True):
             pair = pairs[b]
             flat = pair["st"][:].rearrange("p k (e s) -> p (k e) s", e=2)
             mean, m2 = flat[:, :, 1], flat[:, :, 2]
@@ -198,9 +205,9 @@ def tile_tabnet_glu_step_f2_kernel(
             def times(out, in0, in1):
                 nc.vector.tensor_tensor(out=tile(out), in0=in0, in1=in1, op=MULT)
 
-            def step(out, in0, in1):
+            def stt(out, in0, number, op0, in1):
                 nc.vector.scalar_tensor_tensor(
-                    out=tile(out), in0=pair[in0][:], scalar=20.0 / 9.0, in1=pair[in1][:], op0=ADD, op1=MULT
+                    out=tile(out), in0=pair[in0][:], scalar=number, in1=pair[in1][:], op0=op0, op1=MULT
                 )
 
             cols = slice(16 * (2 * (b // (2 * CHUNKS)) + b % 2), 16 * (2 * (b // (2 * CHUNKS)) + b % 2) + 16)
@@ -217,47 +224,64 @@ def tile_tabnet_glu_step_f2_kernel(
                     scalar1=1, scalar2=0x3FFFFFFF, op0=SHR, op1=XOR,
                 ),
                 lambda: times("w1", pair["p1"][:], pair["v"][:]),
-                lambda: step("y1", "s1", "y0"),
+                lambda: stt("y1", "s1", 20.0 / 9.0, ADD, "y0"),
                 lambda: times("w2", pair["p2"][:], pair["v"][:]),
-                lambda: step("y2", "s2", "y1"),
+                lambda: stt("y2", "s2", 20.0 / 9.0, ADD, "y1"),
                 lambda: times("mul", pair["y2"][:], gain[:, cols]),
                 lambda: times("moved", mean, pair["mul"][:]),
                 lambda: nc.vector.tensor_tensor(out=tile("off"), in0=shift[:, cols], in1=pair["moved"][:], op=SUB),
             ]
-            return on_act, on_dve
+            if both:
+                return on_act, on_dve
+            alone = [
+                lambda: nc.vector.tensor_scalar(
+                    out=tile("v"), in0=m2, scalar1=1.0 / V, scalar2=EPS, op0=MULT, op1=ADD
+                ),
+                on_dve[0],
+                lambda: stt("p1", "y0", K1, MULT, "y0"),
+                on_dve[1],
+                lambda: stt("s1", "w1", 10.0 / 3.0, SUB, "w1"),
+                lambda: stt("y1", "s1", 5.0, ADD, "y0"),
+                lambda: stt("p2", "y1", K2, MULT, "y1"),
+                on_dve[3],
+                lambda: stt("s2", "w2", 10.0 / 3.0, SUB, "w2"),
+                lambda: stt("y2", "s2", 5.0, ADD, "y1"),
+            ]
+            return [], alone + on_dve[5:]
 
-        def act(u):
+        def sig(u, j):
             mul, off = pairs[u // 2]["mul"], pairs[u // 2]["off"]
-            gate = work.tile([P, 512], F32, name="gate")
-            lin = work.tile([P, 512], F32, name="lin")
-            state[u]["gate"], state[u]["lin"] = gate, lin
+            if j == 0:
+                state[u]["gate"] = work.tile([P, 512], F32, bufs=4, name="gate")
+            k = 8 * (u % 2) + j
+            nc.scalar.activation(
+                out=state[u]["gate"][:, P * j : P * j + P], in_=state[u][0][:, P * j : P * j + P],
+                func=SIGMOID, scale=mul[:, k : k + 1], bias=off[:, k : k + 1],
+            )
 
-            def block(half, j):
-                k = 8 * (u % 2) + 4 * half + j
-                nc.scalar.activation(
-                    out=(gate, lin)[half][:, P * j : P * j + P],
-                    in_=state[u]["banks"][half][:, P * j : P * j + P],
-                    func=(SIGMOID, IDENTITY)[half],
-                    scale=mul[:, k : k + 1],
-                    bias=off[:, k : k + 1],
+        def affine(u, j, on_act):
+            mul, off = pairs[u // 2]["mul"], pairs[u // 2]["off"]
+            k = 8 * (u % 2) + 4 + j
+            raw = state[u]["raw"][:, P * j : P * j + P]
+            if on_act:
+                nc.scalar.activation(out=raw, in_=raw, func=IDENTITY, scale=mul[:, k : k + 1], bias=off[:, k : k + 1])
+            else:
+                nc.vector.tensor_scalar(
+                    out=raw, in0=raw, scalar1=mul[:, k : k + 1], scalar2=off[:, k : k + 1], op0=MULT, op1=ADD
                 )
 
-            return [lambda half=half, j=j: block(half, j) for half in range(2) for j in range(4)]
-
         def product(u):
+            prod = work.tile([P, 512], F32, bufs=5, name="prod")
+            state[u]["prod"] = prod
+            nc.vector.tensor_tensor(out=prod[:], in0=state[u]["gate"][:], in1=state[u]["raw"][:], op=MULT)
+
+        def skipped(u):
             stage, s0, g, c = where(u)
-            if stage == 0:
-                dst = h_all[:, c : c + 2, s0 : s0 + C]
-            else:
-                prod = work.tile([P, 512], F32, name="prod")
-                state[u]["prod"] = prod
-                dst = prod[:].rearrange("p (c s) -> p c s", c=2)
-            nc.vector.tensor_tensor(
-                out=dst,
-                in0=state[u]["gate"][:].rearrange("p (c s) -> p c s", c=2),
-                in1=state[u]["lin"][:].rearrange("p (c s) -> p c s", c=2),
-                op=MULT,
-            )
+            for q in range(2):
+                nc.vector.tensor_scalar_mul(
+                    hs_all[:, c + q, s0 : s0 + C], state[u]["prod"][:, C * q : C * q + C],
+                    vec[:, 64 + c + q : 65 + c + q],
+                )
 
         def spread(u):
             stage, s0, g, c = where(u)
@@ -268,7 +292,7 @@ def tile_tabnet_glu_step_f2_kernel(
                 for t in range(4):
                     nc.sync.dma_start(
                         out=pairs[u // 2]["pre"][32 * r : 32 * r + 32, t, :],
-                        in_=h_all[t:P:4, c + q, s0 : s0 + C],
+                        in_=state[u]["prod"][t:P:4, C * q : C * q + C],
                     )
 
         def group(b):
@@ -288,33 +312,25 @@ def tile_tabnet_glu_step_f2_kernel(
                 in_=pairs[b]["grouped"][:].rearrange("p n t -> p (n t)"),
             )
 
-        def final(u):
+        def turn(u, ended=False):
             stage, s0, g, c = where(u)
-            y = work.tile([P, 512], F32, name="y")
-            for q in range(2):
-                cols = slice(q * C, (q + 1) * C)
-                nc.vector.scalar_tensor_tensor(
-                    out=y[:, cols],
-                    in0=h_all[:, c + q, s0 : s0 + C],
-                    scalar=vec[:, 64 + c + q : 65 + c + q],
-                    in1=state[u]["prod"][:, cols],
-                    op0=MULT,
-                    op1=ADD,
-                )
-            state[u]["y"] = y
-
-        def turn(u):
-            bank = psum.tile([P, 512], F32, tag="tr", bufs=1, name="turned")
+            if ended:
+                bank = psum.tile([P, 512], F32, tag="gate", name="turned")
+            else:
+                bank = psum.tile([P, 512], F32, tag="turned", bufs=1, name="turned")
             for v in range(2):
                 for q in range(2):
-                    nc.tensor.transpose(
-                        bank[:, P * (2 * v + q) : P * (2 * v + q) + P],
-                        state[u]["y"][:, q * C + V * v : q * C + V * v + V],
-                        ident[:],
-                    )
+                    out = bank[:, P * (2 * v + q) : P * (2 * v + q) + P]
+                    for i, src in enumerate(
+                        (
+                            state[u]["prod"][:, q * C + V * v : q * C + V * v + V],
+                            hs_all[:, c + q, s0 + V * v : s0 + V * v + V],
+                        )
+                    ):
+                        nc.tensor.matmul(out, lhsT=src, rhs=ident[:], start=(i == 0), stop=(i == 1), is_transpose=True)
             state[u]["turned"] = bank
 
-        def leave(u):
+        def leave(u, on_act=True):
             stage, s0, g, c = where(u)
             v0 = s0 // V
             turned = state[u]["turned"][:].rearrange("p (v c) -> p v c", v=2)
@@ -326,95 +342,108 @@ def tile_tabnet_glu_step_f2_kernel(
                     out=res_v, in0=turned, scalar=0.0,
                     in1=dp[:, v0 : v0 + 2, col : col + 2 * P], op0=MAX, op1=ADD,
                 )
-            else:
+            elif on_act:
                 nc.scalar.copy(out=res_v, in_=turned)
+            else:
+                nc.vector.tensor_copy(out=res_v, in_=turned)
             nc.sync.dma_start(
                 out=(out_0, out_1)[g][s0 : s0 + C, col : col + 2 * P].rearrange("(v s) c -> s v c", s=V),
                 in_=res_v,
             )
 
-        urgent = []
-        waiting = []
-        emitted = set()
+        for u, half in ((0, 1), (0, 0), (1, 1), (1, 0)):
+            mm(u, half)
+        units = 2 * STEPS
+        for w in range(STEPS):
+            a, d, p = [[[] for r in range(8)] for engine in range(3)]
 
-        def emit(queue, count):
-            for i in range(min(count, len(queue))):
-                queue.pop(0)()
+            def put(queue, r, fn, *args):
+                queue[r].append((fn, args))
 
-        def emit_act(count):
-            for i in range(count):
-                emit(urgent if urgent else waiting, 1)
+            def pair_of(step):
+                return [2 * step, 2 * step + 1] if 0 <= step < STEPS else []
 
-        def need(key):
-            while key not in emitted:
-                emit_act(1)
-
-        def mark(key, work_item):
-            work_item()
-            emitted.add(key)
-
-        def quant_when_grouped(b):
-            need(("group", b))
-            quant(b)
-
-        def finish(u):
-            final(u)
-            turn(u)
-            if where(u)[2] == 1:
-                urgent.append(lambda: leave(u))
-
-        def multiply(u):
-            need(("act", u))
-            product(u)
-            if u < STEPS:
-                spread(u)
-
-        mm(0)
-        mm(1)
-        load_vectors(0)
-        for part in range(8):
-            stats(part // 4, part % 4)
-        load_vectors(1)
-        mm(2)
-        mm(3)
-        for b in range(STEPS + 3):
-            dve = []
-            ahead = []
-            if b + 1 < STEPS:
-                for part in range(8):
-                    ahead.append(lambda u=2 * b + 2 + part // 4, part=part % 4: stats(u, part))
-            for half in range(2):
-                end, new, old = 2 * b - 4 + half, 2 * b + 2 + half, 2 * b - 2 + half
-                ending = STEPS <= end < 2 * STEPS
-                if ending:
-                    dve.append(lambda u=end: finish(u))
-                if 4 <= new < 2 * STEPS:
-                    dve.append(lambda u=new: mm(u))
-                if 0 <= old < 2 * STEPS:
-                    if not ending:
-                        dve += ahead[:EARLY]
-                        ahead = ahead[EARLY:]
-                    dve.append(lambda u=old: multiply(u))
-                if ending and where(end)[2] == 0:
-                    dve.append(lambda u=end: leave(u))
-            if 0 <= b - 3 < STEPS // 2:
-                waiting.append(lambda b=b: mark(("group", b - 3), lambda: group(b - 3)))
-                dve.append(lambda b=b: quant_when_grouped(b - 3))
-            dve += ahead
-            if b < STEPS:
-                on_act, on_dve = chain(b)
-                for r in range(8):
-                    emit(on_act, 1)
-                    emit_act(2)
-                    emit(dve, 1)
+            second = w >= STEPS // 2
+            for i, u in enumerate(pair_of(w)):
+                put(a, (0, 5 if second else 4)[i], take, u)
+                put(d, (0, 4 if second else 3)[i], stats, u, 1)
+                put(d, (1, 3 if second else 6)[i], stats, u, 0)
+            if second and w < STEPS:
+                put(p, 1, mm, 2 * w + 1, 1)
+            for i, u in enumerate(pair_of(w + 1)):
+                if u < STEPS:
+                    put(p, PL1 + 2 * i, mm, u, 1)
+                    put(p, PL1 + 1 + 2 * i, mm, u, 0)
+                else:
+                    put(p, 2 + 2 * i, mm, u, 0)
+                    if i == 0:
+                        put(p, 6, mm, u, 1)
+            for i, u in enumerate(pair_of(w - 2)):
+                for j in range(4):
+                    put(a, 2 * i + j // 2, sig, u, j)
+                    if j < (AFF_S1 if u < STEPS else AFF_EVEN if w % 2 else AFF_ODD):
+                        put(a, 4 + i, affine, u, j, True)
+                    else:
+                        put(d, 4, affine, u, j, False)
+                put(d, (5, 7)[i], product, u)
+                if u < STEPS:
+                    put(d, (5, 7)[i], spread, u)
+            for i, u in enumerate(pair_of(w - 3)):
+                if u < STEPS:
+                    put(d, (2, 2)[i], skipped, u)
+                else:
+                    put(p, 4 * i, turn, u)
+                    if where(u)[2] == 0:
+                        put(d, (2, 6)[i], leave, u)
+                    else:
+                        put(a, (3, 7)[i], leave, u)
+            if 0 <= w - 3 < STEPS // 2:
+                put(a, 6, group, w - 3)
+            if 0 <= w - 4 < STEPS // 2:
+                put(d, 1, quant, w - 4)
+            on_act, on_dve = chain(w - 1) if w else ([], [])
+            if w == 0:
+                put(p, 5, load_vectors, 0)
+            if w == 1:
+                put(d, 3, load_vectors, 1)
+            for r in range(8):
+                for fn, args in a[r][:1]:
+                    fn(*args)
+                if r < len(on_act):
+                    on_act[r]()
+                for fn, args in a[r][1:] + p[r] + d[r]:
+                    fn(*args)
+                if on_dve:
                     on_dve[r]()
-                for u in (2 * b, 2 * b + 1):
-                    blocks = act(u)
-                    waiting += blocks[:-1]
-                    waiting.append(lambda u=u, last=blocks[-1]: mark(("act", u), last))
-                while dve:
-                    emit(dve, 1)
-                    emit_act(RATE)
-            else:
-                emit(dve, 99)
-                emit_act(99)
+
+        last = STEPS - 1
+        for u in pair_of(last - 2):
+            turn(u, True)
+        for u in pair_of(last - 1):
+            for j in range(4):
+                sig(u, j)
+        fill = []
+        for u in pair_of(last - 1):
+            for j in range(0, 4, 2):
+                fill.append(lambda u=u, j=j: [affine(u, j, False), affine(u, j + 1, False)])
+        for u in pair_of(last - 1):
+            fill.append(lambda u=u: [product(u), turn(u, True)])
+        for i, small in enumerate(chain(last, both=False)[1]):
+            small()
+            for item in fill[i : i + 1]:
+                item()
+        for u in pair_of(last - 2):
+            leave(u)
+        for u in pair_of(last):
+            for j in range(4):
+                sig(u, j)
+        for u in pair_of(last):
+            for j in range(4):
+                affine(u, j, False)
+        for u in pair_of(last - 1):
+            leave(u)
+        for u in pair_of(last):
+            product(u)
+            turn(u, True)
+        for i, u in enumerate(pair_of(last)):
+            leave(u, i == 0)

@@ -24,7 +24,7 @@ SHR = mybir.AluOpType.logical_shift_right
 XOR = mybir.AluOpType.bitwise_xor
 SIGMOID = mybir.ActivationFunctionType.Sigmoid
 IDENTITY = mybir.ActivationFunctionType.Identity
-SQUARE = mybir.ActivationFunctionType.Square
+COPY = mybir.ActivationFunctionType.Copy
 
 K1 = 2.0**124.87
 K2 = K1 * (3.0 / 8.0) ** 2
@@ -37,10 +37,7 @@ C = 256
 CHUNKS = M // C
 STEPS = 2 * CHUNKS * 2
 ACT_GROUPS = True
-AFF_S1 = 1
-AFF_EVEN = 4
-AFF_ODD = 0
-PL1 = 3
+ORDER = {"first":{"share":2,"dve":["L0a","L0b","G0a","G0b","A0","Q","L1a","L1b","A1","P0","G1a","G1b","P1"],"act":["S00","S01","S02 T0","S03","S10 A00","S11","S12","S13","A10 T1","","R","",""],"pe":["","","","","","","L0","G0","","L1","G1","",""]},"short":{"share":2,"dve":["L0a","L0b","Q","G0a","G0b","A0 A1","G1a","G1b","L1a","L1b","P0","P1",""],"act":["S00","S01","S02 T0","S03","S10 A00","S11 A01","S12 A10","S13 A11","H00 H01","T1","R H10 H11","",""],"pe":["","","N","G0","","","","","G1","","","L0",""]},"even":{"share":4,"dve":["L0a","L0b Q","G0a","G0b","K0","G1a","G1b","L1a","L1b","P0","","P1","K1"],"act":["S00","","S01 S02 T0","S03","S10 A00","S11 A01","A10","S13 A11","H00 S12","T1","H10 H11","H01",""],"pe":["U0","","N","G0","","","","U1","G1","","","L0",""]},"odd":{"share":2,"dve":["","L0b L0a","G0a","G0b","A0 H0","G1a","G1b","L1a","L1b","P0","A1 H1","","P1"],"act":["S00","S01","S02 T0","S03","S10 A00","S11 K0","S12 A10","S13","","T1","","K1",""],"pe":["U0","","N","G0","","","","U1","G1","","","L0",""]}}
 
 
 def tile_tabnet_glu_step_f2_kernel(
@@ -68,7 +65,7 @@ def tile_tabnet_glu_step_f2_kernel(
         shift = keep.tile([P, 64], F32, name="shift")
         warm = keep.tile([P, 1], F32, name="warm")
         dp = keep.tile([P, M // V, D], BF16, name="dp")
-        hs_all = keep.tile([P, N // P, M], F32, name="hs_all")
+        h_all = keep.tile([P, N // P, M], F32, name="h_all")
         hc = keep.tile([P, GN, M], U32, align_bytes=64, name="hc")
         hs = keep.tile([P, GN, M], U8, align_bytes=64, name="hs")
 
@@ -180,74 +177,52 @@ def tile_tabnet_glu_step_f2_kernel(
             state[u]["raw"] = work.tile([P, 512], F32, bufs=7, name="raw")
             nc.scalar.copy(out=state[u]["raw"][:], in_=state[u][1][:])
 
-        def stats(u, half):
+        def stats(u, half, q):
             pair = pairs[u // 2]
             if "st" not in pair:
                 pair["st"] = work.tile([P, 8, 6], F32, name="st")
-            for q in range(2):
-                nc.vector.bn_stats(
-                    out=pair["st"][:, 4 * (u % 2) + 2 * half + q, :],
-                    in_=state[u][half][:, C * q : C * q + C].rearrange("p (e s) -> p s e", e=2),
-                )
+            nc.vector.bn_stats(
+                out=pair["st"][:, 4 * (u % 2) + 2 * half + q, :],
+                in_=state[u][half][:, C * q : C * q + C].rearrange("p (e s) -> p s e", e=2),
+            )
 
-        def chain(b, both=True):
+        def chain(b):
             pair = pairs[b]
             flat = pair["st"][:].rearrange("p k (e s) -> p (k e) s", e=2)
             mean, m2 = flat[:, :, 1], flat[:, :, 2]
+            first = 16 * (2 * (b // (2 * CHUNKS)) + b % 2)
+            cols = slice(first, first + 16)
 
             def tile(name):
                 pair[name] = work.tile([P, 16], F32, name="chain_" + name)
                 return pair[name][:]
-
-            def square(out, in_, scale, bias):
-                nc.scalar.activation(out=tile(out), in_=pair[in_][:], func=SQUARE, scale=scale, bias=bias)
-
-            def times(out, in0, in1):
-                nc.vector.tensor_tensor(out=tile(out), in0=in0, in1=in1, op=MULT)
 
             def stt(out, in0, number, op0, in1):
                 nc.vector.scalar_tensor_tensor(
                     out=tile(out), in0=pair[in0][:], scalar=number, in1=pair[in1][:], op0=op0, op1=MULT
                 )
 
-            cols = slice(16 * (2 * (b // (2 * CHUNKS)) + b % 2), 16 * (2 * (b // (2 * CHUNKS)) + b % 2) + 16)
-            on_act = [
-                lambda: nc.scalar.activation(out=tile("v"), in_=m2, func=IDENTITY, scale=1.0 / V, bias=EPS),
-                lambda: square("p1", "y0", K1**0.5, 0.0),
-                lambda: square("s1", "w1", 1.0, -5.0 / 3.0),
-                lambda: square("p2", "y1", K2**0.5, 0.0),
-                lambda: square("s2", "w2", 1.0, -5.0 / 3.0),
-            ]
-            on_dve = [
+            def tt(out, in0, in1, op):
+                nc.vector.tensor_tensor(out=tile(out), in0=in0, in1=in1, op=op)
+
+            return [
+                lambda: nc.vector.tensor_scalar(out=tile("v"), in0=m2, scalar1=1.0 / V, scalar2=EPS, op0=MULT, op1=ADD),
                 lambda: nc.vector.tensor_scalar(
                     out=tile("y0").bitcast(I32), in0=pair["v"][:].bitcast(I32),
                     scalar1=1, scalar2=0x3FFFFFFF, op0=SHR, op1=XOR,
                 ),
-                lambda: times("w1", pair["p1"][:], pair["v"][:]),
-                lambda: stt("y1", "s1", 20.0 / 9.0, ADD, "y0"),
-                lambda: times("w2", pair["p2"][:], pair["v"][:]),
-                lambda: stt("y2", "s2", 20.0 / 9.0, ADD, "y1"),
-                lambda: times("mul", pair["y2"][:], gain[:, cols]),
-                lambda: times("moved", mean, pair["mul"][:]),
-                lambda: nc.vector.tensor_tensor(out=tile("off"), in0=shift[:, cols], in1=pair["moved"][:], op=SUB),
-            ]
-            if both:
-                return on_act, on_dve
-            alone = [
-                lambda: nc.vector.tensor_scalar(
-                    out=tile("v"), in0=m2, scalar1=1.0 / V, scalar2=EPS, op0=MULT, op1=ADD
-                ),
-                on_dve[0],
                 lambda: stt("p1", "y0", K1, MULT, "y0"),
-                on_dve[1],
+                lambda: tt("w1", pair["p1"][:], pair["v"][:], MULT),
                 lambda: stt("s1", "w1", 10.0 / 3.0, SUB, "w1"),
                 lambda: stt("y1", "s1", 5.0, ADD, "y0"),
                 lambda: stt("p2", "y1", K2, MULT, "y1"),
-                on_dve[3],
+                lambda: tt("w2", pair["p2"][:], pair["v"][:], MULT),
                 lambda: stt("s2", "w2", 10.0 / 3.0, SUB, "w2"),
                 lambda: stt("y2", "s2", 5.0, ADD, "y1"),
+                lambda: tt("mul", pair["y2"][:], gain[:, cols], MULT),
+                lambda: tt("moved", mean, pair["mul"][:], MULT),
+                lambda: tt("off", shift[:, cols], pair["moved"][:], SUB),
             ]
-            return [], alone + on_dve[5:]
 
         def sig(u, j):
             mul, off = pairs[u // 2]["mul"], pairs[u // 2]["off"]
@@ -260,6 +235,7 @@ def tile_tabnet_glu_step_f2_kernel(
             )
 
         def affine(u, j, on_act):
+            state[u]["lines"] = state[u].get("lines", 0) + 1
             mul, off = pairs[u // 2]["mul"], pairs[u // 2]["off"]
             k = 8 * (u % 2) + 4 + j
             raw = state[u]["raw"][:, P * j : P * j + P]
@@ -271,17 +247,30 @@ def tile_tabnet_glu_step_f2_kernel(
                 )
 
         def product(u):
-            prod = work.tile([P, 512], F32, bufs=5, name="prod")
-            state[u]["prod"] = prod
-            nc.vector.tensor_tensor(out=prod[:], in0=state[u]["gate"][:], in1=state[u]["raw"][:], op=MULT)
-
-        def skipped(u):
+            assert state[u]["lines"] == 4
             stage, s0, g, c = where(u)
-            for q in range(2):
-                nc.vector.tensor_scalar_mul(
-                    hs_all[:, c + q, s0 : s0 + C], state[u]["prod"][:, C * q : C * q + C],
-                    vec[:, 64 + c + q : 65 + c + q],
-                )
+            if stage == 0:
+                dst = h_all[:, c : c + 2, s0 : s0 + C]
+            else:
+                state[u]["prod"] = work.tile([P, 512], F32, bufs=5, name="prod")
+                dst = state[u]["prod"][:].rearrange("p (c s) -> p c s", c=2)
+            nc.vector.tensor_tensor(
+                out=dst,
+                in0=state[u]["gate"][:].rearrange("p (c s) -> p c s", c=2),
+                in1=state[u]["raw"][:].rearrange("p (c s) -> p c s", c=2),
+                op=MULT,
+            )
+
+        def skipped(u, q, on_act):
+            stage, s0, g, c = where(u)
+            if q == 0:
+                state[u]["hs"] = work.tile([P, 512], F32, bufs=5, name="hs_skip")
+            dst, src = state[u]["hs"][:, C * q : C * q + C], h_all[:, c + q, s0 : s0 + C]
+            factor = vec[:, 64 + c + q : 65 + c + q]
+            if on_act:
+                nc.scalar.activation(out=dst, in_=src, func=COPY, scale=factor)
+            else:
+                nc.vector.tensor_scalar_mul(dst, src, factor)
 
         def spread(u):
             stage, s0, g, c = where(u)
@@ -292,7 +281,7 @@ def tile_tabnet_glu_step_f2_kernel(
                 for t in range(4):
                     nc.sync.dma_start(
                         out=pairs[u // 2]["pre"][32 * r : 32 * r + 32, t, :],
-                        in_=state[u]["prod"][t:P:4, C * q : C * q + C],
+                        in_=h_all[t:P:4, c + q, s0 : s0 + C],
                     )
 
         def group(b):
@@ -324,7 +313,7 @@ def tile_tabnet_glu_step_f2_kernel(
                     for i, src in enumerate(
                         (
                             state[u]["prod"][:, q * C + V * v : q * C + V * v + V],
-                            hs_all[:, c + q, s0 + V * v : s0 + V * v + V],
+                            state[u]["hs"][:, q * C + V * v : q * C + V * v + V],
                         )
                     ):
                         nc.tensor.matmul(out, lhsT=src, rhs=ident[:], start=(i == 0), stop=(i == 1), is_transpose=True)
@@ -334,7 +323,7 @@ def tile_tabnet_glu_step_f2_kernel(
             stage, s0, g, c = where(u)
             v0 = s0 // V
             turned = state[u]["turned"][:].rearrange("p (v c) -> p v c", v=2)
-            res = work.tile([P, 512], F32, name="res")
+            res = work.tile([P, 512], F32, bufs=6, name="res")
             res_v = res[:].rearrange("p (v c) -> p v c", v=2)
             col = P * c % D
             if g == 0:
@@ -353,68 +342,79 @@ def tile_tabnet_glu_step_f2_kernel(
 
         for u, half in ((0, 1), (0, 0), (1, 1), (1, 0)):
             mm(u, half)
-        units = 2 * STEPS
+
+        def pair_of(step):
+            return [2 * step, 2 * step + 1] if 0 <= step < STEPS else []
+
+        def dve_item(w, code):
+            kind, rest = code[0], code[1:]
+            if kind in "LG":
+                u = 2 * w + int(rest[0])
+                stats(u, 1 if kind == "L" else 0, "ab".index(rest[1]))
+            elif kind == "A" and w >= 2:
+                u = 2 * (w - 2) + int(rest[0])
+                for j in range(ORDER[type_of(w)]["share"], 4):
+                    affine(u, j, False)
+            elif kind == "P" and w >= 2:
+                u = 2 * (w - 2) + int(rest[0])
+                product(u)
+                if u < STEPS:
+                    spread(u)
+            elif kind == "Q" and 0 <= w - 4 < STEPS // 2:
+                quant(w - 4)
+            elif kind == "K" and w - 3 >= STEPS // 2:
+                leave(2 * (w - 3) + int(rest[0]))
+            elif kind == "H" and w - 2 >= STEPS // 2:
+                for q in range(2):
+                    skipped(2 * (w - 2) + int(rest[0]), q, False)
+
+        def act_item(w, code):
+            kind, rest = code[0], code[1:]
+            if kind == "T":
+                take(2 * w + int(rest[0]))
+            elif kind == "S" and w >= 2:
+                sig(2 * (w - 2) + int(rest[0]), int(rest[1]))
+            elif kind == "A" and w >= 2:
+                u = 2 * (w - 2) + int(rest[0])
+                for j in range(2 * int(rest[1]), min(2 * int(rest[1]) + 2, ORDER[type_of(w)]["share"])):
+                    affine(u, j, True)
+            elif kind == "R" and 0 <= w - 3 < STEPS // 2:
+                group(w - 3)
+            elif kind == "K" and w - 3 >= STEPS // 2:
+                leave(2 * (w - 3) + int(rest[0]))
+            elif kind == "H" and w - 2 >= STEPS // 2:
+                skipped(2 * (w - 2) + int(rest[0]), int(rest[1]), True)
+
+        def pe_item(w, code):
+            kind, rest = code[0], code[1:]
+            if kind == "N" and w >= STEPS // 2:
+                mm(2 * w + 1, 1)
+            elif kind in "LG" and w + 1 < STEPS:
+                u = 2 * (w + 1) + int(rest[0])
+                if not (u >= STEPS and code == "L1"):
+                    mm(u, 1 if kind == "L" else 0)
+            elif kind == "U" and w - 3 >= STEPS // 2:
+                turn(2 * (w - 3) + int(rest[0]))
+
+        def type_of(w):
+            return "first" if w < 6 else "short" if w < 9 else "even" if w % 2 else "odd"
+
         for w in range(STEPS):
-            a, d, p = [[[] for r in range(8)] for engine in range(3)]
-
-            def put(queue, r, fn, *args):
-                queue[r].append((fn, args))
-
-            def pair_of(step):
-                return [2 * step, 2 * step + 1] if 0 <= step < STEPS else []
-
-            second = w >= STEPS // 2
-            for i, u in enumerate(pair_of(w)):
-                put(a, (0, 5 if second else 4)[i], take, u)
-                put(d, (0, 4 if second else 3)[i], stats, u, 1)
-                put(d, (1, 3 if second else 6)[i], stats, u, 0)
-            if second and w < STEPS:
-                put(p, 1, mm, 2 * w + 1, 1)
-            for i, u in enumerate(pair_of(w + 1)):
-                if u < STEPS:
-                    put(p, PL1 + 2 * i, mm, u, 1)
-                    put(p, PL1 + 1 + 2 * i, mm, u, 0)
-                else:
-                    put(p, 2 + 2 * i, mm, u, 0)
-                    if i == 0:
-                        put(p, 6, mm, u, 1)
-            for i, u in enumerate(pair_of(w - 2)):
-                for j in range(4):
-                    put(a, 2 * i + j // 2, sig, u, j)
-                    if j < (AFF_S1 if u < STEPS else AFF_EVEN if w % 2 else AFF_ODD):
-                        put(a, 4 + i, affine, u, j, True)
-                    else:
-                        put(d, 4, affine, u, j, False)
-                put(d, (5, 7)[i], product, u)
-                if u < STEPS:
-                    put(d, (5, 7)[i], spread, u)
-            for i, u in enumerate(pair_of(w - 3)):
-                if u < STEPS:
-                    put(d, (2, 2)[i], skipped, u)
-                else:
-                    put(p, 4 * i, turn, u)
-                    if where(u)[2] == 0:
-                        put(d, (2, 6)[i], leave, u)
-                    else:
-                        put(a, (3, 7)[i], leave, u)
-            if 0 <= w - 3 < STEPS // 2:
-                put(a, 6, group, w - 3)
-            if 0 <= w - 4 < STEPS // 2:
-                put(d, 1, quant, w - 4)
-            on_act, on_dve = chain(w - 1) if w else ([], [])
-            if w == 0:
-                put(p, 5, load_vectors, 0)
-            if w == 1:
-                put(d, 3, load_vectors, 1)
-            for r in range(8):
-                for fn, args in a[r][:1]:
-                    fn(*args)
-                if r < len(on_act):
-                    on_act[r]()
-                for fn, args in a[r][1:] + p[r] + d[r]:
-                    fn(*args)
-                if on_dve:
-                    on_dve[r]()
+            order = ORDER[type_of(w)]
+            smalls = chain(w - 1) if w else []
+            for r, codes in enumerate(order["dve"]):
+                for code in order["act"][r].split():
+                    act_item(w, code)
+                for code in order["pe"][r].split():
+                    pe_item(w, code)
+                for code in codes.split():
+                    dve_item(w, code)
+                if w == 0 and r == 10:
+                    load_vectors(0)
+                if w == 1 and r == 6:
+                    load_vectors(1)
+                for small in smalls[r : r + 1]:
+                    small()
 
         last = STEPS - 1
         for u in pair_of(last - 2):
@@ -424,11 +424,12 @@ def tile_tabnet_glu_step_f2_kernel(
                 sig(u, j)
         fill = []
         for u in pair_of(last - 1):
-            for j in range(0, 4, 2):
-                fill.append(lambda u=u, j=j: [affine(u, j, False), affine(u, j + 1, False)])
-        for u in pair_of(last - 1):
+            fill += [lambda u=u, q=q: skipped(u, q, False) for q in range(2)]
+            fill.append(lambda u=u: [affine(u, j, False) for j in range(4)])
             fill.append(lambda u=u: [product(u), turn(u, True)])
-        for i, small in enumerate(chain(last, both=False)[1]):
+        for u in pair_of(last):
+            fill += [lambda u=u, q=q: skipped(u, q, False) for q in range(2)]
+        for i, small in enumerate(chain(last)):
             small()
             for item in fill[i : i + 1]:
                 item()
@@ -440,10 +441,9 @@ def tile_tabnet_glu_step_f2_kernel(
         for u in pair_of(last):
             for j in range(4):
                 affine(u, j, False)
-        for u in pair_of(last - 1):
-            leave(u)
-        for u in pair_of(last):
+        for u, before in zip(pair_of(last), pair_of(last - 1)):
             product(u)
             turn(u, True)
+            leave(before)
         for i, u in enumerate(pair_of(last)):
             leave(u, i == 0)

@@ -3,7 +3,11 @@ from contextlib import ExitStack
 import concourse.mybir as mybir
 from concourse.masks import make_identity
 
-M, K, N, D, V = 768, 1536, 1024, 512, 128
+M = 768
+K = 1536
+N = 1024
+D = 512
+V = 128
 EPS = 1e-3
 ROOT_HALF = 0.5**0.5
 
@@ -17,27 +21,97 @@ U8 = mybir.dt.uint8
 FP8X4 = mybir.dt.float8_e4m3fn_x4
 FP4X4 = mybir.dt.float4_e2m1fn_x4
 ADD = mybir.AluOpType.add
-MULT = mybir.AluOpType.mult
 SUB = mybir.AluOpType.subtract
+MULT = mybir.AluOpType.mult
 MAX = mybir.AluOpType.max
-SHR = mybir.AluOpType.logical_shift_right
+SHIFT_RIGHT = mybir.AluOpType.logical_shift_right
 XOR = mybir.AluOpType.bitwise_xor
 SIGMOID = mybir.ActivationFunctionType.Sigmoid
 IDENTITY = mybir.ActivationFunctionType.Identity
 COPY = mybir.ActivationFunctionType.Copy
-
-K1 = 2.0**124.87
-K2 = K1 * (3.0 / 8.0) ** 2
-K3 = K1**0.5 * (3.0 / 8.0) ** 2
+SQRT = mybir.ActivationFunctionType.Sqrt
 
 P = 128
-GK = K // 512
-GN = N // 512
-C = 256
-CHUNKS = M // C
-STEPS = 2 * CHUNKS * 2
-ACT_GROUPS = True
-ORDER = {"first":{"share":2,"dve":["L0a","L0b","G0a","G0b","A0","Q","L1a","L1b","A1","P0","G1a","G1b","P1"],"act":["S00","S01","S02 T0","S03","S10 A00","S11","S12","S13","A10 T1","","R","",""],"pe":["","","","","","","L0","G0","","L1","G1","",""]},"short":{"share":2,"dve":["L0a","L0b","Q","G0a","G0b","A0 A1","G1a","G1b","L1a","L1b","P0","P1",""],"act":["S00","S01","S02 T0","S03","S10 A00","S11 A01","S12 A10","S13 A11","H00 H01","T1","R H10 H11","",""],"pe":["","","N","G0","","","","","G1","","","L0",""]},"even":{"share":4,"dve":["L0a","L0b Q","G0a","G0b","K0","G1a","G1b","L1a","L1b","P0","","P1","K1"],"act":["S00","","S01 S02 T0","S03","S10 A00","S11 A01","A10","S13 A11","H00 S12","T1","H10 H11","H01",""],"pe":["U0","","N","G0","","","","U1","G1","","","L0",""]},"odd":{"share":2,"dve":["","L0b L0a","G0a","G0b","A0 H0","G1a","G1b","L1a","L1b","P0","A1 H1","","P1"],"act":["S00","S01","S02 T0","S03","S10 A00","S11 K0","S12 A10","S13","","T1","","K1",""],"pe":["U0","","N","G0","","","","U1","G1","","","L0",""]}}
+K_PASS = 512
+A_PASSES = K // K_PASS
+B_PASSES = N // K_PASS
+CHUNK = 256
+UNIT = 2 * CHUNK
+BLOCKS = 16
+STAGE_STEPS = 2 * (M // CHUNK)
+STEPS = 2 * STAGE_STEPS
+GATE, LINEAR = 0, 1
+TURN_FROM = STAGE_STEPS + 3
+
+SEED_MASK = 0x3FFFFFFF
+SEED_SQUARE = 2.0**124.87
+REFINED_SQUARE = SEED_SQUARE * (3.0 / 8.0) ** 2
+SEED_SCALE = SEED_SQUARE**0.5 * (3.0 / 8.0) ** 2
+
+FIRST = (
+    ("sigmoid 0 0", "", "stats linear 0 0"),
+    ("sigmoid 0 1", "", "stats linear 0 1"),
+    ("sigmoid 0 2, take 0", "", "stats gate 0 0"),
+    ("sigmoid 0 3, affine 0 0", "", "stats gate 0 1"),
+    ("affine 0 1, sigmoid 1 0", "", "quantise"),
+    ("sigmoid 1 1", "matmul linear 0", "stats linear 1 0"),
+    ("sigmoid 1 2", "", "stats linear 1 1"),
+    ("sigmoid 1 3, affine 1 0", "matmul gate 0", "product 0"),
+    ("take 1, affine 1 1", "matmul linear 1", "stats gate 1 0"),
+    ("interleave", "matmul gate 1", "stats gate 1 1"),
+    ("skip 0 0, skip 0 1, skip 1 0, skip 1 1", "", "product 1"),
+    ("", "", ""),
+)
+DECISION = (
+    ("sigmoid 0 0", "turn 0", "stats linear 0 0"),
+    ("sigmoid 0 1", "", "stats linear 0 1, quantise"),
+    ("sigmoid 0 2, take 0", "late linear 1", "leave 0"),
+    ("sigmoid 0 3", "matmul gate 0", "stats gate 0 0"),
+    ("sigmoid 1 0, affine 0 0", "turn 1", "stats gate 0 1"),
+    ("sigmoid 1 1, affine 0 1", "", "stats gate 1 0"),
+    ("sigmoid 1 2, affine 1 0", "", "stats linear 1 0"),
+    ("sigmoid 1 3", "matmul gate 1", "stats linear 1 1"),
+    ("take 1, affine 1 1", "", "stats gate 1 1"),
+    ("skip 0 0, skip 0 1", "matmul linear 0", "product 0"),
+    ("skip 1 0, skip 1 1", "", "product 1"),
+    ("", "", "leave 1"),
+)
+ATTENTION = (
+    ("sigmoid 0 0", "turn 0", "stats linear 0 0"),
+    ("sigmoid 0 1", "", "stats linear 0 1"),
+    ("sigmoid 0 2, take 0", "late linear 1", "stats gate 0 0"),
+    ("leave 0", "matmul gate 0", "stats gate 0 1"),
+    ("sigmoid 0 3, sigmoid 1 0", "", "skip 0 0, skip 0 1"),
+    ("sigmoid 1 1, affine 0 0", "turn 1", "stats gate 1 0"),
+    ("affine 0 1, sigmoid 1 2", "", "stats linear 1 0"),
+    ("sigmoid 1 3", "matmul gate 1", "stats linear 1 1"),
+    ("take 1, affine 1 0", "", "stats gate 1 1"),
+    ("affine 1 1", "matmul linear 0", "product 0"),
+    ("leave 1", "", "skip 1 0, skip 1 1"),
+    ("", "", "product 1"),
+)
+LAST = (
+    ("sigmoid 0 0", "turn 0", "stats linear 0 0"),
+    ("sigmoid 0 1", "", "stats linear 0 1"),
+    ("sigmoid 0 2, take 0", "late linear 1", "leave 0"),
+    ("sigmoid 0 3", "", "stats gate 0 0"),
+    ("sigmoid 1 0, affine 0 0", "turn 1", "stats gate 0 1"),
+    ("sigmoid 1 1, affine 0 1, sigmoid 1 2", "", "stats gate 1 0"),
+    ("sigmoid 1 3, affine 1 0", "", "stats linear 1 0"),
+    ("affine 1 1, sqrt table", "", "stats linear 1 1"),
+    ("take 1", "", "stats gate 1 1"),
+    ("", "", "product 0"),
+    ("", "", "product 1"),
+    ("", "", "leave 1"),
+)
+
+
+def window_order(w):
+    if w < TURN_FROM:
+        return FIRST
+    if w == STEPS - 1:
+        return LAST
+    return ATTENTION if (w - 3) % 2 else DECISION
 
 
 def tile_tabnet_glu_step_f2_kernel(
@@ -51,399 +125,417 @@ def tile_tabnet_glu_step_f2_kernel(
         psum = ctx.enter_context(tc.psum_pool(name="psum", bufs=6))
         ctx.enter_context(tc.manual_schedule())
 
-        xt_w = keep.tile([P, GK, 2 * M], U8, align_bytes=64, name="xt_w")
-        xt_s = keep.tile([P, GK, M], U8, align_bytes=64, name="xt_s")
-        a_w = keep.tile([P, GK, 4 * N], U8, align_bytes=64, name="a_w")
-        a_s = keep.tile([P, GK, 2 * N], U8, align_bytes=64, name="a_s")
-        b_w = keep.tile([P, GN, 4 * N], U8, align_bytes=64, name="b_w")
-        b_s = keep.tile([P, GN, 2 * N], U8, align_bytes=64, name="b_s")
-        vec_in = keep.tile([P, P], BF16, name="vec_in")
-        ident_bf = keep.tile([P, P], BF16, name="ident_bf")
-        vec = keep.tile([P, P], F32, name="vec")
-        ident = keep.tile([P, P], F32, name="ident")
-        gain = keep.tile([P, 64], F32, name="gain")
-        shift = keep.tile([P, 64], F32, name="shift")
-        warm = keep.tile([P, 1], F32, name="warm")
-        dp = keep.tile([P, M // V, D], BF16, name="dp")
+        xt_w = keep.tile([P, A_PASSES, 2 * M], U8, align_bytes=64, name="xt_w")
+        xt_s = keep.tile([P, A_PASSES, M], U8, align_bytes=64, name="xt_s")
+        a_w = keep.tile([P, A_PASSES, 4 * N], U8, align_bytes=64, name="a_w")
+        a_s = keep.tile([P, A_PASSES, 2 * N], U8, align_bytes=64, name="a_s")
+        b_w = keep.tile([P, B_PASSES, 4 * N], U8, align_bytes=64, name="b_w")
+        b_s = keep.tile([P, B_PASSES, 2 * N], U8, align_bytes=64, name="b_s")
+        h_codes = keep.tile([P, B_PASSES, M], U32, align_bytes=64, name="h_codes")
+        h_scales = keep.tile([P, B_PASSES, M], U8, align_bytes=64, name="h_scales")
         h_all = keep.tile([P, N // P, M], F32, name="h_all")
-        hc = keep.tile([P, GN, M], U32, align_bytes=64, name="hc")
-        hs = keep.tile([P, GN, M], U8, align_bytes=64, name="hs")
+        vector_rows = [keep.tile([P, P], BF16, name="vector_rows%d" % stage) for stage in range(2)]
+        vectors = [keep.tile([P, P], F32, name="vectors%d" % stage) for stage in range(2)]
+        gain = keep.tile([P, 4 * BLOCKS], F32, name="gain")
+        shift = keep.tile([P, 4 * BLOCKS], F32, name="shift")
+        skip_factor = keep.tile([P, N // P], F32, name="skip_factor")
+        ident = keep.tile([P, P], F32, name="ident")
+        ident_bf = keep.tile([P, P], BF16, name="ident_bf")
+        d_tile = keep.tile([P, M // V, D], BF16, name="d_tile")
+        one_column = keep.tile([P, 1], F32, name="one_column")
 
-        nc.vector.memset(warm[:], 0.0)
         nc.vector.memset(xt_s[:].rearrange("p g n -> p (g n)").bitcast(I32), 0)
         nc.vector.memset(a_s[:].rearrange("p g n -> p (g n)").bitcast(I32), 0)
-        nc.vector.memset(vec_in[:], 0.0)
+        nc.vector.memset(one_column[:], 0.0)
         nc.vector.memset(b_s[:].rearrange("p g n -> p (g n)").bitcast(I32), 0)
-        nc.scalar.activation(out=warm[:], in_=warm[:], func=SIGMOID)
+        nc.scalar.activation(out=one_column[:], in_=one_column[:], func=SIGMOID)
 
         def load_scales(plane, src):
-            for q in range(4):
+            for quadrant in range(4):
                 nc.sync.dma_start(
-                    out=plane[32 * q : 32 * q + 4, :, :].bitcast(I32),
-                    in_=src[:, 4 * q : 4 * q + 4, :].rearrange("g q n -> q g n").bitcast(I32),
+                    out=plane[32 * quadrant : 32 * quadrant + 4, :, :].bitcast(I32),
+                    in_=src[:, 4 * quadrant : 4 * quadrant + 4, :].rearrange("g q n -> q g n").bitcast(I32),
                 )
 
-        def load_words(tile, src, c0, c1, queue=nc.sync):
-            queue.dma_start(
-                out=tile[:, :, c0:c1].bitcast(I32),
-                in_=src[:, :, c0:c1].rearrange("g p n -> p g n").bitcast(I32),
+        def load_words(tile, src, first, last):
+            nc.sync.dma_start(
+                out=tile[:, :, first:last].bitcast(I32),
+                in_=src[:, :, first:last].rearrange("g p n -> p g n").bitcast(I32),
             )
 
-        load_words(xt_w, xt_words, 0, 512, nc.gpsimd)
-        load_words(a_w, a_words, 2 * N, 2 * N + 512, nc.gpsimd)
-        load_words(a_w, a_words, 0, 512, nc.gpsimd)
+        def load_vector_rows(stage, sources):
+            row = 0
+            for source in sources:
+                rows = source.shape[0] // P
+                nc.gpsimd.dma_start(
+                    out=vector_rows[stage][row : row + rows, :], in_=source.rearrange("(c p) -> c p", p=P)
+                )
+                row += rows
+
+        for stage in range(2):
+            nc.gpsimd.memset(vector_rows[stage][:].bitcast(I32), 0)
+        load_vector_rows(0, (gain1, shift1))
         make_identity(nc, ident[:])
-        row = 0
-        for v in (gain1, shift1, gain2, shift2, skip):
-            rows = v.shape[0] // P
-            nc.gpsimd.dma_start(out=vec_in[row : row + rows, :], in_=v.rearrange("(c p) -> c p", p=P))
-            row += rows
+        nc.vector.tensor_copy(out=ident_bf[:], in_=ident[:])
         load_scales(xt_s, xt_scales)
         load_scales(a_s, a_scales)
+        tile_bytes = 2 * P
+        linear_bytes = 2 * N
+        load_words(a_w, a_words, linear_bytes, linear_bytes + 2 * tile_bytes)
+        load_words(xt_w, xt_words, 0, 2 * CHUNK)
+        load_words(a_w, a_words, 0, 2 * tile_bytes)
         for c0, c1 in ((2, 4), (4, 8)):
-            load_words(a_w, a_words, 2 * N + 256 * c0, 2 * N + 256 * c1)
-            load_words(a_w, a_words, 256 * c0, 256 * c1)
-        load_words(xt_w, xt_words, 512, 1536)
-        load_scales(b_s, b_scales)
+            load_words(a_w, a_words, linear_bytes + tile_bytes * c0, linear_bytes + tile_bytes * c1)
+            load_words(a_w, a_words, tile_bytes * c0, tile_bytes * c1)
+        load_words(xt_w, xt_words, 2 * CHUNK, 2 * M)
         load_words(b_w, b_words, 0, 4 * N)
-        nc.sync.dma_start(out=dp[:], in_=d_prev.rearrange("(v s) c -> s v c", s=V))
+        load_scales(b_s, b_scales)
+        nc.sync.dma_start(out=d_tile[:], in_=d_prev.rearrange("(v s) c -> s v c", s=V))
 
-        nc.vector.tensor_copy(out=ident_bf[:], in_=ident[:])
-        vec_ps = psum.tile([P, 1024], BF16, tag="gate", name="vec_ps")
+        def turn_vectors(stage):
+            bank = psum.tile([P, 2 * UNIT], BF16, tag="gate", name="vector_bank")
+            nc.tensor.transpose(bank[:, 0:P], vector_rows[stage][:], ident_bf[:])
+            return bank
 
-        def load_vectors(part):
-            if part == 0:
-                nc.tensor.transpose(vec_ps[:, 0:P], vec_in[:], ident_bf[:])
-                return
-            nc.vector.tensor_copy(out=vec[:], in_=vec_ps[:, 0:P])
-            for stage in range(2):
-                for dst, base, factor in ((gain, 32 * stage, K3), (shift, 32 * stage + 16, 1.0)):
-                    for half in range(2):
-                        f = factor * (ROOT_HALF if stage and half else 1.0)
-                        cols = vec[:, base + 8 * half : base + 8 * half + 8]
-                        spread_to = dst[:, 32 * stage : 32 * stage + 32]
-                        spread_to = spread_to.rearrange("p (u h c v) -> p h u c v", u=4, h=2, c=2)
-                        nc.gpsimd.tensor_scalar(
-                            out=spread_to[:, half, :, :, :],
-                            in0=cols.rearrange("p (u c o) -> p u c o", u=4, o=1).to_broadcast([P, 4, 2, 2]),
-                            scalar1=f, scalar2=0.0, op0=MULT, op1=ADD,
-                        )
-            nc.gpsimd.tensor_scalar(
-                out=vec[:, 64:72], in0=vec[:, 64:72], scalar1=ROOT_HALF, scalar2=0.0, op0=MULT, op1=ADD
-            )
-
-        def where(u):
-            b, half = divmod(u, 2)
-            stage, rest = divmod(b, 2 * CHUNKS)
-            chunk, g = divmod(rest, 2)
-            return stage, C * chunk, g, 4 * g + 2 * half
-
-        state = [dict() for u in range(2 * STEPS)]
-        pairs = [dict() for b in range(STEPS)]
-
-        def mm(u, half):
-            stage, s0, g_, c = where(u)
-            if half == 0:
-                bank = psum.tile([P, 512], F32, tag="gate", name="bank")
-            elif stage == 0 and u % 2:
-                bank = psum.tile([P, 512], F32, tag="turned", bufs=1, name="bank")
-            else:
-                bank = psum.tile([P, 512], F32, tag="linear", bufs=1, name="bank")
-            state[u][half] = bank
-            words, scales, mov, mov_s, passes, width = (
-                (a_w, a_s, xt_w, xt_s, GK, 256) if stage == 0 else (b_w, b_s, hc, hs, GN, 128)
-            )
-            for q in range(2):
-                col = half * N + P * (c + q)
-                for r in range(0, C, width):
-                    m0 = s0 + r
-                    for g in range(passes):
-                        rhs = (
-                            mov[:, g, 2 * m0 : 2 * (m0 + width)].bitcast(FP4X4)
-                            if stage == 0
-                            else mov[:, g, m0 : m0 + width].bitcast(FP8X4)
-                        )
-                        nc.tensor.matmul_mx(
-                            out=bank[:, q * C + r : q * C + r + width],
-                            lhsT=words[:, g, 2 * col : 2 * col + 2 * P].bitcast(FP4X4),
-                            lhsT_scale=scales[:, g, col : col + P],
-                            rhs=rhs,
-                            rhs_scale=mov_s[:, g, m0 : m0 + width],
-                            start=(g == 0),
-                            stop=(g == passes - 1),
-                        )
-
-        def take(u):
-            state[u]["raw"] = work.tile([P, 512], F32, bufs=7, name="raw")
-            nc.scalar.copy(out=state[u]["raw"][:], in_=state[u][1][:])
-
-        def stats(u, half, q):
-            pair = pairs[u // 2]
-            if "st" not in pair:
-                pair["st"] = work.tile([P, 8, 6], F32, name="st")
-            nc.vector.bn_stats(
-                out=pair["st"][:, 4 * (u % 2) + 2 * half + q, :],
-                in_=state[u][half][:, C * q : C * q + C].rearrange("p (e s) -> p s e", e=2),
-            )
-
-        def chain(b):
-            pair = pairs[b]
-            flat = pair["st"][:].rearrange("p k (e s) -> p (k e) s", e=2)
-            mean, m2 = flat[:, :, 1], flat[:, :, 2]
-            first = 16 * (2 * (b // (2 * CHUNKS)) + b % 2)
-            cols = slice(first, first + 16)
-
-            def tile(name):
-                pair[name] = work.tile([P, 16], F32, name="chain_" + name)
-                return pair[name][:]
-
-            def stt(out, in0, number, op0, in1):
-                nc.vector.scalar_tensor_tensor(
-                    out=tile(out), in0=pair[in0][:], scalar=number, in1=pair[in1][:], op0=op0, op1=MULT
+        def spread_vectors(stage, bank):
+            nc.vector.tensor_copy(out=vectors[stage][:], in_=bank[:, 0:P])
+            for dst, first_row, factor in ((gain, 0, SEED_SCALE), (shift, 16, 1.0)):
+                for half in (GATE, LINEAR):
+                    columns = vectors[stage][:, first_row + 8 * half : first_row + 8 * half + 8]
+                    blocks = dst[:, 2 * BLOCKS * stage : 2 * BLOCKS * (stage + 1)]
+                    blocks = blocks.rearrange("p (u h c v) -> p h u c v", u=4, h=2, c=2)
+                    nc.gpsimd.tensor_scalar(
+                        out=blocks[:, half, :, :, :],
+                        in0=columns.rearrange("p (u c o) -> p u c o", u=4, o=1).to_broadcast([P, 4, 2, 2]),
+                        scalar1=factor * (ROOT_HALF if stage and half == LINEAR else 1.0),
+                        scalar2=0.0,
+                        op0=MULT,
+                        op1=ADD,
+                    )
+            if stage:
+                nc.gpsimd.tensor_scalar(
+                    out=skip_factor[:], in0=vectors[1][:, 32:40], scalar1=ROOT_HALF, scalar2=0.0, op0=MULT, op1=ADD
                 )
 
-            def tt(out, in0, in1, op):
-                nc.vector.tensor_tensor(out=tile(out), in0=in0, in1=in1, op=op)
+        def place(u):
+            step, unit = divmod(u, 2)
+            stage, rest = divmod(step, STAGE_STEPS)
+            chunk, g = divmod(rest, 2)
+            return stage, CHUNK * chunk, g, 4 * g + 2 * unit
 
+        def of_step(step):
+            return [2 * step, 2 * step + 1] if 0 <= step < STEPS else []
+
+        units = [dict() for u in range(2 * STEPS)]
+        steps = [dict() for step in range(STEPS)]
+
+        def multiply(u, half):
+            stage, s0, g, c = place(u)
+            if half == GATE:
+                bank = psum.tile([P, UNIT], F32, tag="gate", name="gate_bank")
+            elif u % 2 and u // 2 < TURN_FROM:
+                bank = psum.tile([P, UNIT], F32, tag="turned", bufs=1, name="second_linear_bank")
+            else:
+                bank = psum.tile([P, UNIT], F32, tag="linear", bufs=1, name="linear_bank")
+            units[u][half] = bank
+            words, scales, passes, width = (a_w, a_s, A_PASSES, CHUNK) if stage == 0 else (b_w, b_s, B_PASSES, V)
+            for q in range(2):
+                column = half * N + P * (c + q)
+                for start in range(0, CHUNK, width):
+                    samples = slice(s0 + start, s0 + start + width)
+                    for k_pass in range(passes):
+                        if stage == 0:
+                            moving = xt_w[:, k_pass, 2 * samples.start : 2 * samples.stop].bitcast(FP4X4)
+                            moving_scales = xt_s[:, k_pass, samples]
+                        else:
+                            moving = h_codes[:, k_pass, samples].bitcast(FP8X4)
+                            moving_scales = h_scales[:, k_pass, samples]
+                        nc.tensor.matmul_mx(
+                            out=bank[:, q * CHUNK + start : q * CHUNK + start + width],
+                            lhsT=words[:, k_pass, 2 * column : 2 * (column + P)].bitcast(FP4X4),
+                            lhsT_scale=scales[:, k_pass, column : column + P],
+                            rhs=moving,
+                            rhs_scale=moving_scales,
+                            start=(k_pass == 0),
+                            stop=(k_pass == passes - 1),
+                        )
+
+        def statistics(u, half, q):
+            step = steps[u // 2]
+            if "stats" not in step:
+                step["stats"] = work.tile([P, 8, 6], F32, name="stats")
+            nc.vector.bn_stats(
+                out=step["stats"][:, 4 * (u % 2) + 2 * half + q, :],
+                in_=units[u][half][:, CHUNK * q : CHUNK * (q + 1)].rearrange("p (v s) -> p s v", v=2),
+            )
+
+        def moments(step):
+            blocks = steps[step]["stats"][:].rearrange("p k (v x) -> p (k v) x", v=2)
+            return blocks[:, :, 1], blocks[:, :, 2]
+
+        def levels(step, rooted=False):
+            tiles = steps[step]
+            mean, count_variance = moments(step)
+            first = BLOCKS * (2 * (step // STAGE_STEPS) + step % 2)
+            gains, shifts = gain[:, first : first + BLOCKS], shift[:, first : first + BLOCKS]
+
+            def new(name):
+                tiles[name] = work.tile([P, BLOCKS], F32, name="level_" + name)
+                return tiles[name][:]
+
+            def combine(name, in0, number, op, in1):
+                nc.vector.scalar_tensor_tensor(out=new(name), in0=in0, scalar=number, in1=in1, op0=op, op1=MULT)
+
+            def binary(name, in0, in1, op):
+                nc.vector.tensor_tensor(out=new(name), in0=in0, in1=in1, op=op)
+
+            def at(name):
+                return tiles[name][:]
+
+            def variance():
+                nc.vector.tensor_scalar(
+                    out=new("var"), in0=count_variance, scalar1=1.0 / V, scalar2=EPS, op0=MULT, op1=ADD
+                )
+
+            def seed():
+                nc.vector.tensor_scalar(
+                    out=new("y0").bitcast(I32), in0=at("var").bitcast(I32),
+                    scalar1=1, scalar2=SEED_MASK, op0=SHIFT_RIGHT, op1=XOR,
+                )
+
+            def offset():
+                binary("offset", shifts, at("moved"), SUB)
+
+            if rooted:
+                return [
+                    lambda: nc.vector.reciprocal(out=new("inverse"), in_=at("root")),
+                    lambda: combine("scale", at("inverse"), 1.0 / SEED_SCALE, MULT, gains),
+                    lambda: binary("moved", mean, at("scale"), MULT),
+                    offset,
+                ]
             return [
-                lambda: nc.vector.tensor_scalar(out=tile("v"), in0=m2, scalar1=1.0 / V, scalar2=EPS, op0=MULT, op1=ADD),
-                lambda: nc.vector.tensor_scalar(
-                    out=tile("y0").bitcast(I32), in0=pair["v"][:].bitcast(I32),
-                    scalar1=1, scalar2=0x3FFFFFFF, op0=SHR, op1=XOR,
+                variance,
+                seed,
+                lambda: combine("square1", at("y0"), SEED_SQUARE, MULT, at("y0")),
+                lambda: binary("w1", at("square1"), at("var"), MULT),
+                lambda: combine("quadratic1", at("w1"), 10.0 / 3.0, SUB, at("w1")),
+                lambda: combine("y1", at("quadratic1"), 5.0, ADD, at("y0")),
+                lambda: combine("square2", at("y1"), REFINED_SQUARE, MULT, at("y1")),
+                lambda: binary("w2", at("square2"), at("var"), MULT),
+                lambda: (
+                    combine("quadratic2", at("w2"), 10.0 / 3.0, SUB, at("w2")),
+                    binary("mean_gain", mean, gains, MULT),
                 ),
-                lambda: stt("p1", "y0", K1, MULT, "y0"),
-                lambda: tt("w1", pair["p1"][:], pair["v"][:], MULT),
-                lambda: stt("s1", "w1", 10.0 / 3.0, SUB, "w1"),
-                lambda: stt("y1", "s1", 5.0, ADD, "y0"),
-                lambda: stt("p2", "y1", K2, MULT, "y1"),
-                lambda: tt("w2", pair["p2"][:], pair["v"][:], MULT),
-                lambda: stt("s2", "w2", 10.0 / 3.0, SUB, "w2"),
-                lambda: stt("y2", "s2", 5.0, ADD, "y1"),
-                lambda: tt("mul", pair["y2"][:], gain[:, cols], MULT),
-                lambda: tt("moved", mean, pair["mul"][:], MULT),
-                lambda: tt("off", shift[:, cols], pair["moved"][:], SUB),
+                lambda: combine("y2", at("quadratic2"), 5.0, ADD, at("y1")),
+                lambda: (
+                    binary("scale", at("y2"), gains, MULT),
+                    binary("moved", at("y2"), at("mean_gain"), MULT),
+                ),
+                offset,
             ]
 
-        def sig(u, j):
-            mul, off = pairs[u // 2]["mul"], pairs[u // 2]["off"]
+        def take(u):
+            units[u]["linear"] = work.tile([P, UNIT], F32, bufs=7, name="linear_half")
+            nc.scalar.copy(out=units[u]["linear"][:], in_=units[u][LINEAR][:])
+
+        def scale_and_offset(u, half, j):
+            block = 8 * (u % 2) + 4 * half + j
+            return [steps[u // 2][name][:, block : block + 1] for name in ("scale", "offset")]
+
+        def sigmoid(u, j):
             if j == 0:
-                state[u]["gate"] = work.tile([P, 512], F32, bufs=4, name="gate")
-            k = 8 * (u % 2) + j
+                units[u]["sigmoid"] = work.tile([P, UNIT], F32, bufs=4, name="sigmoid_half")
+            scale, offset = scale_and_offset(u, GATE, j)
             nc.scalar.activation(
-                out=state[u]["gate"][:, P * j : P * j + P], in_=state[u][0][:, P * j : P * j + P],
-                func=SIGMOID, scale=mul[:, k : k + 1], bias=off[:, k : k + 1],
+                out=units[u]["sigmoid"][:, V * j : V * (j + 1)], in_=units[u][GATE][:, V * j : V * (j + 1)],
+                func=SIGMOID, scale=scale, bias=offset,
             )
 
-        def affine(u, j, on_act):
-            state[u]["lines"] = state[u].get("lines", 0) + 1
-            mul, off = pairs[u // 2]["mul"], pairs[u // 2]["off"]
-            k = 8 * (u % 2) + 4 + j
-            raw = state[u]["raw"][:, P * j : P * j + P]
-            if on_act:
-                nc.scalar.activation(out=raw, in_=raw, func=IDENTITY, scale=mul[:, k : k + 1], bias=off[:, k : k + 1])
+        def affine(u, j, on_scalar):
+            scale, offset = scale_and_offset(u, LINEAR, j)
+            block = units[u]["linear"][:, V * j : V * (j + 1)]
+            if on_scalar:
+                nc.scalar.activation(out=block, in_=block, func=IDENTITY, scale=scale, bias=offset)
             else:
-                nc.vector.tensor_scalar(
-                    out=raw, in0=raw, scalar1=mul[:, k : k + 1], scalar2=off[:, k : k + 1], op0=MULT, op1=ADD
-                )
+                nc.vector.tensor_scalar(out=block, in0=block, scalar1=scale, scalar2=offset, op0=MULT, op1=ADD)
 
         def product(u):
-            assert state[u]["lines"] == 4
-            stage, s0, g, c = where(u)
+            stage, s0, g, c = place(u)
             if stage == 0:
-                dst = h_all[:, c : c + 2, s0 : s0 + C]
+                dst = h_all[:, c : c + 2, s0 : s0 + CHUNK]
             else:
-                state[u]["prod"] = work.tile([P, 512], F32, bufs=5, name="prod")
-                dst = state[u]["prod"][:].rearrange("p (c s) -> p c s", c=2)
+                units[u]["product"] = work.tile([P, UNIT], F32, bufs=7, name="product_tile")
+                dst = units[u]["product"][:].rearrange("p (c s) -> p c s", c=2)
             nc.vector.tensor_tensor(
                 out=dst,
-                in0=state[u]["gate"][:].rearrange("p (c s) -> p c s", c=2),
-                in1=state[u]["raw"][:].rearrange("p (c s) -> p c s", c=2),
+                in0=units[u]["sigmoid"][:].rearrange("p (c s) -> p c s", c=2),
+                in1=units[u]["linear"][:].rearrange("p (c s) -> p c s", c=2),
                 op=MULT,
             )
+            if stage == 0:
+                if u % 2 == 0:
+                    steps[u // 2]["slots"] = work.tile([P, 4, CHUNK], F32, name="slots")
+                for q in range(2):
+                    first = 32 * ((c + q) % 4)
+                    nc.sync.dma_start(
+                        out=steps[u // 2]["slots"][first : first + 32, :, :].rearrange("p t s -> p (t s)"),
+                        in_=h_all[:, c + q, s0 : s0 + CHUNK],
+                    )
 
-        def skipped(u, q, on_act):
-            stage, s0, g, c = where(u)
+        def interleave(step):
+            steps[step]["grouped"] = work.tile([P, CHUNK, 4], BF16, align_bytes=64, name="grouped")
+            nc.scalar.copy(out=steps[step]["grouped"][:], in_=steps[step]["slots"][:].rearrange("p t s -> p s t"))
+
+        def quantise(step):
+            stage, s0, g, c = place(2 * step)
+            nc.vector.quantize_mx(
+                out=h_codes[:, g, s0 : s0 + CHUNK].bitcast(FP8X4),
+                scales=h_scales[:, g, s0 : s0 + CHUNK],
+                in_=steps[step]["grouped"][:].rearrange("p s t -> p (s t)"),
+            )
+
+        def skip_term(u, q, on_scalar):
+            stage, s0, g, c = place(u)
             if q == 0:
-                state[u]["hs"] = work.tile([P, 512], F32, bufs=5, name="hs_skip")
-            dst, src = state[u]["hs"][:, C * q : C * q + C], h_all[:, c + q, s0 : s0 + C]
-            factor = vec[:, 64 + c + q : 65 + c + q]
-            if on_act:
+                units[u]["skip"] = work.tile([P, UNIT], F32, bufs=7, name="skip_tile")
+            dst = units[u]["skip"][:, CHUNK * q : CHUNK * (q + 1)]
+            src, factor = h_all[:, c + q, s0 : s0 + CHUNK], skip_factor[:, c + q : c + q + 1]
+            if on_scalar:
                 nc.scalar.activation(out=dst, in_=src, func=COPY, scale=factor)
             else:
                 nc.vector.tensor_scalar_mul(dst, src, factor)
 
-        def spread(u):
-            stage, s0, g, c = where(u)
-            if u % 2 == 0:
-                pairs[u // 2]["pre"] = work.tile([P, 4, C], F32, name="pre")
-            for q in range(2):
-                r = (c + q) % 4
-                for t in range(4):
-                    nc.sync.dma_start(
-                        out=pairs[u // 2]["pre"][32 * r : 32 * r + 32, t, :],
-                        in_=h_all[t:P:4, c + q, s0 : s0 + C],
-                    )
-
-        def group(b):
-            grouped = work.tile([P, C, 4], BF16, align_bytes=64, name="grouped")
-            pairs[b]["grouped"] = grouped
-            src = pairs[b]["pre"][:].rearrange("p t n -> p n t")
-            if ACT_GROUPS:
-                nc.scalar.copy(out=grouped[:], in_=src)
+        def turn(u, at_end=False):
+            if at_end:
+                bank = psum.tile([P, UNIT], F32, tag="gate", name="turned_bank")
             else:
-                nc.vector.tensor_copy(out=grouped[:], in_=src)
-
-        def quant(b):
-            stage, s0, g, c = where(2 * b)
-            nc.vector.quantize_mx(
-                out=hc[:, g, s0 : s0 + C].bitcast(FP8X4),
-                scales=hs[:, g, s0 : s0 + C],
-                in_=pairs[b]["grouped"][:].rearrange("p n t -> p (n t)"),
-            )
-
-        def turn(u, ended=False):
-            stage, s0, g, c = where(u)
-            if ended:
-                bank = psum.tile([P, 512], F32, tag="gate", name="turned")
-            else:
-                bank = psum.tile([P, 512], F32, tag="turned", bufs=1, name="turned")
+                bank = psum.tile([P, UNIT], F32, tag="turned", bufs=1, name="turned_bank")
+            units[u]["turned"] = bank
             for v in range(2):
                 for q in range(2):
-                    out = bank[:, P * (2 * v + q) : P * (2 * v + q) + P]
-                    for i, src in enumerate(
-                        (
-                            state[u]["prod"][:, q * C + V * v : q * C + V * v + V],
-                            state[u]["hs"][:, q * C + V * v : q * C + V * v + V],
+                    block = slice(CHUNK * q + V * v, CHUNK * q + V * (v + 1))
+                    for name in ("product", "skip"):
+                        nc.tensor.matmul(
+                            bank[:, P * (2 * v + q) : P * (2 * v + q + 1)],
+                            lhsT=units[u][name][:, block],
+                            rhs=ident[:],
+                            start=(name == "product"),
+                            stop=(name == "skip"),
+                            is_transpose=True,
                         )
-                    ):
-                        nc.tensor.matmul(out, lhsT=src, rhs=ident[:], start=(i == 0), stop=(i == 1), is_transpose=True)
-            state[u]["turned"] = bank
 
-        def leave(u, on_act=True):
-            stage, s0, g, c = where(u)
-            v0 = s0 // V
-            turned = state[u]["turned"][:].rearrange("p (v c) -> p v c", v=2)
-            res = work.tile([P, 512], F32, bufs=6, name="res")
-            res_v = res[:].rearrange("p (v c) -> p v c", v=2)
-            col = P * c % D
+        def leave(u, on_scalar=True):
+            stage, s0, g, c = place(u)
+            turned = units[u]["turned"][:].rearrange("p (v c) -> p v c", v=2)
+            result = work.tile([P, UNIT], F32, bufs=6, name="result")
+            rows = result[:].rearrange("p (v c) -> p v c", v=2)
+            column = P * c % D
             if g == 0:
                 nc.vector.scalar_tensor_tensor(
-                    out=res_v, in0=turned, scalar=0.0,
-                    in1=dp[:, v0 : v0 + 2, col : col + 2 * P], op0=MAX, op1=ADD,
+                    out=rows, in0=turned, scalar=0.0,
+                    in1=d_tile[:, s0 // V : s0 // V + 2, column : column + 2 * P],
+                    op0=MAX, op1=ADD,
                 )
-            elif on_act:
-                nc.scalar.copy(out=res_v, in_=turned)
+            elif on_scalar:
+                nc.scalar.copy(out=rows, in_=turned)
             else:
-                nc.vector.tensor_copy(out=res_v, in_=turned)
+                nc.vector.tensor_copy(out=rows, in_=turned)
             nc.sync.dma_start(
-                out=(out_0, out_1)[g][s0 : s0 + C, col : col + 2 * P].rearrange("(v s) c -> s v c", s=V),
-                in_=res_v,
+                out=(out_0, out_1)[g][s0 : s0 + CHUNK, column : column + 2 * P].rearrange("(v s) c -> s v c", s=V),
+                in_=rows,
             )
 
-        for u, half in ((0, 1), (0, 0), (1, 1), (1, 0)):
-            mm(u, half)
+        def issue(w, item, on_scalar):
+            name, numbers = item.split()[0], [int(x) for x in item.split() if x in ("0", "1", "2", "3")]
+            half = GATE if "gate" in item else LINEAR
+            unit = numbers[0] if numbers else 0
+            now, soon, before, out = [2 * (w + lag) + unit for lag in (0, 1, -2, -3)]
+            if name == "stats":
+                statistics(now, half, numbers[1])
+            elif name == "take":
+                take(now)
+            elif name == "late":
+                multiply(now, LINEAR)
+            elif name == "matmul" and soon < 2 * STEPS:
+                if half == GATE or unit == 0 or w + 1 < TURN_FROM:
+                    multiply(soon, half)
+            elif name == "sigmoid" and before >= 0:
+                sigmoid(before, numbers[1])
+            elif name == "affine" and before >= 0:
+                for j in range(2 * numbers[1], 2 * numbers[1] + 2):
+                    affine(before, j, on_scalar)
+            elif name == "product" and before >= 0:
+                product(before)
+            elif name == "skip" and before >= 2 * STAGE_STEPS:
+                skip_term(before, numbers[1], on_scalar)
+            elif name == "interleave" and 0 <= w - 3 < STAGE_STEPS:
+                interleave(w - 3)
+            elif name == "quantise" and 0 <= w - 4 < STAGE_STEPS:
+                quantise(w - 4)
+            elif name == "turn" and out >= 2 * STAGE_STEPS:
+                turn(out)
+            elif name == "leave" and out >= 2 * STAGE_STEPS:
+                leave(out)
+            elif name == "sqrt":
+                nc.scalar.activation(out=one_column[:], in_=one_column[:], func=SQRT)
 
-        def pair_of(step):
-            return [2 * step, 2 * step + 1] if 0 <= step < STEPS else []
-
-        def dve_item(w, code):
-            kind, rest = code[0], code[1:]
-            if kind in "LG":
-                u = 2 * w + int(rest[0])
-                stats(u, 1 if kind == "L" else 0, "ab".index(rest[1]))
-            elif kind == "A" and w >= 2:
-                u = 2 * (w - 2) + int(rest[0])
-                for j in range(ORDER[type_of(w)]["share"], 4):
-                    affine(u, j, False)
-            elif kind == "P" and w >= 2:
-                u = 2 * (w - 2) + int(rest[0])
-                product(u)
-                if u < STEPS:
-                    spread(u)
-            elif kind == "Q" and 0 <= w - 4 < STEPS // 2:
-                quant(w - 4)
-            elif kind == "K" and w - 3 >= STEPS // 2:
-                leave(2 * (w - 3) + int(rest[0]))
-            elif kind == "H" and w - 2 >= STEPS // 2:
-                for q in range(2):
-                    skipped(2 * (w - 2) + int(rest[0]), q, False)
-
-        def act_item(w, code):
-            kind, rest = code[0], code[1:]
-            if kind == "T":
-                take(2 * w + int(rest[0]))
-            elif kind == "S" and w >= 2:
-                sig(2 * (w - 2) + int(rest[0]), int(rest[1]))
-            elif kind == "A" and w >= 2:
-                u = 2 * (w - 2) + int(rest[0])
-                for j in range(2 * int(rest[1]), min(2 * int(rest[1]) + 2, ORDER[type_of(w)]["share"])):
-                    affine(u, j, True)
-            elif kind == "R" and 0 <= w - 3 < STEPS // 2:
-                group(w - 3)
-            elif kind == "K" and w - 3 >= STEPS // 2:
-                leave(2 * (w - 3) + int(rest[0]))
-            elif kind == "H" and w - 2 >= STEPS // 2:
-                skipped(2 * (w - 2) + int(rest[0]), int(rest[1]), True)
-
-        def pe_item(w, code):
-            kind, rest = code[0], code[1:]
-            if kind == "N" and w >= STEPS // 2:
-                mm(2 * w + 1, 1)
-            elif kind in "LG" and w + 1 < STEPS:
-                u = 2 * (w + 1) + int(rest[0])
-                if not (u >= STEPS and code == "L1"):
-                    mm(u, 1 if kind == "L" else 0)
-            elif kind == "U" and w - 3 >= STEPS // 2:
-                turn(2 * (w - 3) + int(rest[0]))
-
-        def type_of(w):
-            return "first" if w < 6 else "short" if w < 9 else "even" if w % 2 else "odd"
-
+        spread_vectors(0, turn_vectors(0))
+        for u in of_step(0):
+            multiply(u, LINEAR)
+            multiply(u, GATE)
         for w in range(STEPS):
-            order = ORDER[type_of(w)]
-            smalls = chain(w - 1) if w else []
-            for r, codes in enumerate(order["dve"]):
-                for code in order["act"][r].split():
-                    act_item(w, code)
-                for code in order["pe"][r].split():
-                    pe_item(w, code)
-                for code in codes.split():
-                    dve_item(w, code)
-                if w == 0 and r == 10:
-                    load_vectors(0)
-                if w == 1 and r == 6:
-                    load_vectors(1)
-                for small in smalls[r : r + 1]:
-                    small()
+            between = levels(w - 1) if w else []
+            for r, row in enumerate(window_order(w)):
+                for level in between[r : r + 1]:
+                    level()
+                for engine, items in enumerate(row):
+                    for item in items.split(", "):
+                        if item:
+                            issue(w, item, engine == 0)
+                if w == 2 and r == 1:
+                    load_vector_rows(1, (gain2, shift2, skip))
+                if w == 4 and r == 2:
+                    vector_bank = turn_vectors(1)
+                if w == 4 and r == 9:
+                    spread_vectors(1, vector_bank)
 
         last = STEPS - 1
-        for u in pair_of(last - 2):
-            turn(u, True)
-        for u in pair_of(last - 1):
+        steps[last]["root"] = work.tile([P, BLOCKS], F32, name="root")
+        nc.scalar.activation(
+            out=steps[last]["root"][:], in_=moments(last)[1], func=SQRT, scale=1.0 / V, bias=EPS
+        )
+        nc.scalar.activation(out=one_column[:], in_=one_column[:], func=SIGMOID)
+        between = levels(last, rooted=True)
+        for u in of_step(last - 1):
             for j in range(4):
-                sig(u, j)
-        fill = []
-        for u in pair_of(last - 1):
-            fill += [lambda u=u, q=q: skipped(u, q, False) for q in range(2)]
-            fill.append(lambda u=u: [affine(u, j, False) for j in range(4)])
-            fill.append(lambda u=u: [product(u), turn(u, True)])
-        for u in pair_of(last):
-            fill += [lambda u=u, q=q: skipped(u, q, False) for q in range(2)]
-        for i, small in enumerate(chain(last)):
-            small()
-            for item in fill[i : i + 1]:
-                item()
-        for u in pair_of(last - 2):
-            leave(u)
-        for u in pair_of(last):
-            for j in range(4):
-                sig(u, j)
-        for u in pair_of(last):
+                sigmoid(u, j)
+        for i, u in enumerate(of_step(last - 1)):
             for j in range(4):
                 affine(u, j, False)
-        for u, before in zip(pair_of(last), pair_of(last - 1)):
+            between[2 * i]()
+            for q in range(2):
+                skip_term(u, q, False)
+            between[2 * i + 1]()
+        for u in of_step(last):
+            for j in range(4):
+                sigmoid(u, j)
+        for u in of_step(last):
+            for q in range(2):
+                skip_term(u, q, False)
+        for u in of_step(last - 2):
+            for q in range(2):
+                skip_term(u, q, True)
+        for u in of_step(last - 1):
             product(u)
-            turn(u, True)
-            leave(before)
-        for i, u in enumerate(pair_of(last)):
-            leave(u, i == 0)
+            turn(u, at_end=True)
+        for u, earlier in zip(of_step(last), of_step(last - 1)):
+            for j in range(4):
+                affine(u, j, False)
+            product(u)
+            turn(u, at_end=True)
+            leave(earlier)
+        for u in of_step(last - 2):
+            turn(u, at_end=True)
+        for step in (last, last - 2):
+            for i, u in enumerate(of_step(step)):
+                leave(u, on_scalar=(i == 0))

from contextlib import ExitStack

import concourse.mybir as mybir
from concourse.masks import make_identity

M = 768
K = 1536
N = 1024
D = 512
V = 128
EPS = 1e-3
ROOT_HALF = 0.5**0.5

FLOPS = 2 * M * K * 2 * N + 2 * M * N * 2 * N

F32 = mybir.dt.float32
BF16 = mybir.dt.bfloat16
I32 = mybir.dt.int32
U32 = mybir.dt.uint32
U8 = mybir.dt.uint8
FP8X4 = mybir.dt.float8_e4m3fn_x4
FP4X4 = mybir.dt.float4_e2m1fn_x4
ADD = mybir.AluOpType.add
SUB = mybir.AluOpType.subtract
MULT = mybir.AluOpType.mult
MAX = mybir.AluOpType.max
SHIFT_RIGHT = mybir.AluOpType.logical_shift_right
XOR = mybir.AluOpType.bitwise_xor
SIGMOID = mybir.ActivationFunctionType.Sigmoid
IDENTITY = mybir.ActivationFunctionType.Identity
COPY = mybir.ActivationFunctionType.Copy
SQRT = mybir.ActivationFunctionType.Sqrt

P = 128
K_PASS = 512
A_PASSES = K // K_PASS
B_PASSES = N // K_PASS
CHUNK = 256
UNIT = 2 * CHUNK
BLOCKS = 16
STAGE_STEPS = 2 * (M // CHUNK)
STEPS = 2 * STAGE_STEPS
GATE, LINEAR = 0, 1
TURN_FROM = STAGE_STEPS + 3

SEED_MASK = 0x3FFFFFFF
SEED_SQUARE = 2.0**124.87
REFINED_SQUARE = SEED_SQUARE * (3.0 / 8.0) ** 2
SEED_SCALE = SEED_SQUARE**0.5 * (3.0 / 8.0) ** 2

FIRST = (
    ("sigmoid 0 0", "", "stats linear 0 0"),
    ("sigmoid 0 1", "", "stats linear 0 1"),
    ("sigmoid 0 2, take 0", "", "stats gate 0 0"),
    ("sigmoid 0 3, affine 0 0", "", "stats gate 0 1"),
    ("affine 0 1, sigmoid 1 0", "", "quantise"),
    ("sigmoid 1 1", "matmul linear 0", "stats linear 1 0"),
    ("sigmoid 1 2", "", "stats linear 1 1"),
    ("sigmoid 1 3, affine 1 0", "matmul gate 0", "product 0"),
    ("take 1, affine 1 1", "matmul linear 1", "stats gate 1 0"),
    ("interleave", "matmul gate 1", "stats gate 1 1"),
    ("skip 0 0, skip 0 1, skip 1 0, skip 1 1", "", "product 1"),
    ("", "", ""),
)
DECISION = (
    ("sigmoid 0 0", "turn 0", "stats linear 0 0"),
    ("sigmoid 0 1", "", "stats linear 0 1, quantise"),
    ("sigmoid 0 2, take 0", "late linear 1", "leave 0"),
    ("sigmoid 0 3", "matmul gate 0", "stats gate 0 0"),
    ("sigmoid 1 0, affine 0 0", "turn 1", "stats gate 0 1"),
    ("sigmoid 1 1, affine 0 1", "", "stats gate 1 0"),
    ("sigmoid 1 2, affine 1 0", "", "stats linear 1 0"),
    ("sigmoid 1 3", "matmul gate 1", "stats linear 1 1"),
    ("take 1, affine 1 1", "", "stats gate 1 1"),
    ("skip 0 0, skip 0 1", "matmul linear 0", "product 0"),
    ("skip 1 0, skip 1 1", "", "product 1"),
    ("", "", "leave 1"),
)
ATTENTION = (
    ("sigmoid 0 0", "turn 0", "stats linear 0 0"),
    ("sigmoid 0 1", "", "stats linear 0 1"),
    ("sigmoid 0 2, take 0", "late linear 1", "stats gate 0 0"),
    ("leave 0", "matmul gate 0", "stats gate 0 1"),
    ("sigmoid 0 3, sigmoid 1 0", "", "skip 0 0, skip 0 1"),
    ("sigmoid 1 1, affine 0 0", "turn 1", "stats gate 1 0"),
    ("affine 0 1, sigmoid 1 2", "", "stats linear 1 0"),
    ("sigmoid 1 3", "matmul gate 1", "stats linear 1 1"),
    ("take 1, affine 1 0", "", "stats gate 1 1"),
    ("affine 1 1", "matmul linear 0", "product 0"),
    ("leave 1", "", "skip 1 0, skip 1 1"),
    ("", "", "product 1"),
)
LAST = (
    ("sigmoid 0 0", "turn 0", "stats linear 0 0"),
    ("sigmoid 0 1", "", "stats linear 0 1"),
    ("sigmoid 0 2, take 0", "late linear 1", "leave 0"),
    ("sigmoid 0 3", "", "stats gate 0 0"),
    ("sigmoid 1 0, affine 0 0", "turn 1", "stats gate 0 1"),
    ("sigmoid 1 1, affine 0 1, sigmoid 1 2", "", "stats gate 1 0"),
    ("sigmoid 1 3, affine 1 0", "", "stats linear 1 0"),
    ("affine 1 1, sqrt table", "", "stats linear 1 1"),
    ("take 1", "", "stats gate 1 1"),
    ("", "", "product 0"),
    ("", "", "product 1"),
    ("", "", "leave 1"),
)


def window_order(w):
    if w < TURN_FROM:
        return FIRST
    if w == STEPS - 1:
        return LAST
    return ATTENTION if (w - 3) % 2 else DECISION


def tile_tabnet_glu_step_f2_kernel(
    tc, xt_words, xt_scales, a_words, a_scales, b_words, b_scales,
    gain1, shift1, gain2, shift2, skip, d_prev, out_0, out_1,
):
    nc = tc.nc
    with ExitStack() as ctx:
        keep = ctx.enter_context(tc.tile_pool(name="keep", bufs=1))
        work = ctx.enter_context(tc.tile_pool(name="work", bufs=3))
        psum = ctx.enter_context(tc.psum_pool(name="psum", bufs=6))
        ctx.enter_context(tc.manual_schedule())

        xt_w = keep.tile([P, A_PASSES, 2 * M], U8, align_bytes=64, name="xt_w")
        xt_s = keep.tile([P, A_PASSES, M], U8, align_bytes=64, name="xt_s")
        a_w = keep.tile([P, A_PASSES, 4 * N], U8, align_bytes=64, name="a_w")
        a_s = keep.tile([P, A_PASSES, 2 * N], U8, align_bytes=64, name="a_s")
        b_w = keep.tile([P, B_PASSES, 4 * N], U8, align_bytes=64, name="b_w")
        b_s = keep.tile([P, B_PASSES, 2 * N], U8, align_bytes=64, name="b_s")
        h_codes = keep.tile([P, B_PASSES, M], U32, align_bytes=64, name="h_codes")
        h_scales = keep.tile([P, B_PASSES, M], U8, align_bytes=64, name="h_scales")
        h_all = keep.tile([P, N // P, M], F32, name="h_all")
        vector_rows = [keep.tile([P, P], BF16, name="vector_rows%d" % stage) for stage in range(2)]
        vectors = [keep.tile([P, P], F32, name="vectors%d" % stage) for stage in range(2)]
        gain = keep.tile([P, 4 * BLOCKS], F32, name="gain")
        shift = keep.tile([P, 4 * BLOCKS], F32, name="shift")
        skip_factor = keep.tile([P, N // P], F32, name="skip_factor")
        ident = keep.tile([P, P], F32, name="ident")
        ident_bf = keep.tile([P, P], BF16, name="ident_bf")
        d_tile = keep.tile([P, M // V, D], BF16, name="d_tile")
        one_column = keep.tile([P, 1], F32, name="one_column")

        nc.vector.memset(xt_s[:].rearrange("p g n -> p (g n)").bitcast(I32), 0)
        nc.vector.memset(a_s[:].rearrange("p g n -> p (g n)").bitcast(I32), 0)
        nc.vector.memset(one_column[:], 0.0)
        nc.vector.memset(b_s[:].rearrange("p g n -> p (g n)").bitcast(I32), 0)
        nc.scalar.activation(out=one_column[:], in_=one_column[:], func=SIGMOID)

        def load_scales(plane, src):
            for quadrant in range(4):
                nc.sync.dma_start(
                    out=plane[32 * quadrant : 32 * quadrant + 4, :, :].bitcast(I32),
                    in_=src[:, 4 * quadrant : 4 * quadrant + 4, :].rearrange("g q n -> q g n").bitcast(I32),
                )

        def load_words(tile, src, first, last):
            nc.sync.dma_start(
                out=tile[:, :, first:last].bitcast(I32),
                in_=src[:, :, first:last].rearrange("g p n -> p g n").bitcast(I32),
            )

        def load_vector_rows(stage, sources):
            row = 0
            for source in sources:
                rows = source.shape[0] // P
                nc.gpsimd.dma_start(
                    out=vector_rows[stage][row : row + rows, :], in_=source.rearrange("(c p) -> c p", p=P)
                )
                row += rows

        for stage in range(2):
            nc.gpsimd.memset(vector_rows[stage][:].bitcast(I32), 0)
        load_vector_rows(0, (gain1, shift1))
        make_identity(nc, ident[:])
        nc.vector.tensor_copy(out=ident_bf[:], in_=ident[:])
        load_scales(xt_s, xt_scales)
        load_scales(a_s, a_scales)
        tile_bytes = 2 * P
        linear_bytes = 2 * N
        load_words(a_w, a_words, linear_bytes, linear_bytes + 2 * tile_bytes)
        load_words(xt_w, xt_words, 0, 2 * CHUNK)
        load_words(a_w, a_words, 0, 2 * tile_bytes)
        for c0, c1 in ((2, 4), (4, 8)):
            load_words(a_w, a_words, linear_bytes + tile_bytes * c0, linear_bytes + tile_bytes * c1)
            load_words(a_w, a_words, tile_bytes * c0, tile_bytes * c1)
        load_words(xt_w, xt_words, 2 * CHUNK, 2 * M)
        load_words(b_w, b_words, 0, 4 * N)
        load_scales(b_s, b_scales)
        nc.sync.dma_start(out=d_tile[:], in_=d_prev.rearrange("(v s) c -> s v c", s=V))

        def turn_vectors(stage):
            bank = psum.tile([P, 2 * UNIT], BF16, tag="gate", name="vector_bank")
            nc.tensor.transpose(bank[:, 0:P], vector_rows[stage][:], ident_bf[:])
            return bank

        def spread_vectors(stage, bank):
            nc.vector.tensor_copy(out=vectors[stage][:], in_=bank[:, 0:P])
            for dst, first_row, factor in ((gain, 0, SEED_SCALE), (shift, 16, 1.0)):
                for half in (GATE, LINEAR):
                    columns = vectors[stage][:, first_row + 8 * half : first_row + 8 * half + 8]
                    blocks = dst[:, 2 * BLOCKS * stage : 2 * BLOCKS * (stage + 1)]
                    blocks = blocks.rearrange("p (u h c v) -> p h u c v", u=4, h=2, c=2)
                    nc.gpsimd.tensor_scalar(
                        out=blocks[:, half, :, :, :],
                        in0=columns.rearrange("p (u c o) -> p u c o", u=4, o=1).to_broadcast([P, 4, 2, 2]),
                        scalar1=factor * (ROOT_HALF if stage and half == LINEAR else 1.0),
                        scalar2=0.0,
                        op0=MULT,
                        op1=ADD,
                    )
            if stage:
                nc.gpsimd.tensor_scalar(
                    out=skip_factor[:], in0=vectors[1][:, 32:40], scalar1=ROOT_HALF, scalar2=0.0, op0=MULT, op1=ADD
                )

        def place(u):
            step, unit = divmod(u, 2)
            stage, rest = divmod(step, STAGE_STEPS)
            chunk, g = divmod(rest, 2)
            return stage, CHUNK * chunk, g, 4 * g + 2 * unit

        def of_step(step):
            return [2 * step, 2 * step + 1] if 0 <= step < STEPS else []

        units = [dict() for u in range(2 * STEPS)]
        steps = [dict() for step in range(STEPS)]

        def multiply(u, half):
            stage, s0, g, c = place(u)
            if half == GATE:
                bank = psum.tile([P, UNIT], F32, tag="gate", name="gate_bank")
            elif u % 2 and u // 2 < TURN_FROM:
                bank = psum.tile([P, UNIT], F32, tag="turned", bufs=1, name="second_linear_bank")
            else:
                bank = psum.tile([P, UNIT], F32, tag="linear", bufs=1, name="linear_bank")
            units[u][half] = bank
            words, scales, passes, width = (a_w, a_s, A_PASSES, CHUNK) if stage == 0 else (b_w, b_s, B_PASSES, V)
            for q in range(2):
                column = half * N + P * (c + q)
                for start in range(0, CHUNK, width):
                    samples = slice(s0 + start, s0 + start + width)
                    for k_pass in range(passes):
                        if stage == 0:
                            moving = xt_w[:, k_pass, 2 * samples.start : 2 * samples.stop].bitcast(FP4X4)
                            moving_scales = xt_s[:, k_pass, samples]
                        else:
                            moving = h_codes[:, k_pass, samples].bitcast(FP8X4)
                            moving_scales = h_scales[:, k_pass, samples]
                        nc.tensor.matmul_mx(
                            out=bank[:, q * CHUNK + start : q * CHUNK + start + width],
                            lhsT=words[:, k_pass, 2 * column : 2 * (column + P)].bitcast(FP4X4),
                            lhsT_scale=scales[:, k_pass, column : column + P],
                            rhs=moving,
                            rhs_scale=moving_scales,
                            start=(k_pass == 0),
                            stop=(k_pass == passes - 1),
                        )

        def statistics(u, half, q):
            step = steps[u // 2]
            if "stats" not in step:
                step["stats"] = work.tile([P, 8, 6], F32, name="stats")
            nc.vector.bn_stats(
                out=step["stats"][:, 4 * (u % 2) + 2 * half + q, :],
                in_=units[u][half][:, CHUNK * q : CHUNK * (q + 1)].rearrange("p (v s) -> p s v", v=2),
            )

        def moments(step):
            blocks = steps[step]["stats"][:].rearrange("p k (v x) -> p (k v) x", v=2)
            return blocks[:, :, 1], blocks[:, :, 2]

        def levels(step, rooted=False):
            tiles = steps[step]
            mean, count_variance = moments(step)
            first = BLOCKS * (2 * (step // STAGE_STEPS) + step % 2)
            gains, shifts = gain[:, first : first + BLOCKS], shift[:, first : first + BLOCKS]

            def new(name):
                tiles[name] = work.tile([P, BLOCKS], F32, name="level_" + name)
                return tiles[name][:]

            def combine(name, in0, number, op, in1):
                nc.vector.scalar_tensor_tensor(out=new(name), in0=in0, scalar=number, in1=in1, op0=op, op1=MULT)

            def binary(name, in0, in1, op):
                nc.vector.tensor_tensor(out=new(name), in0=in0, in1=in1, op=op)

            def at(name):
                return tiles[name][:]

            def variance():
                nc.vector.tensor_scalar(
                    out=new("var"), in0=count_variance, scalar1=1.0 / V, scalar2=EPS, op0=MULT, op1=ADD
                )

            def seed():
                nc.vector.tensor_scalar(
                    out=new("y0").bitcast(I32), in0=at("var").bitcast(I32),
                    scalar1=1, scalar2=SEED_MASK, op0=SHIFT_RIGHT, op1=XOR,
                )

            def offset():
                binary("offset", shifts, at("moved"), SUB)

            if rooted:
                return [
                    lambda: nc.vector.reciprocal(out=new("inverse"), in_=at("root")),
                    lambda: combine("scale", at("inverse"), 1.0 / SEED_SCALE, MULT, gains),
                    lambda: binary("moved", mean, at("scale"), MULT),
                    offset,
                ]
            return [
                variance,
                seed,
                lambda: combine("square1", at("y0"), SEED_SQUARE, MULT, at("y0")),
                lambda: binary("w1", at("square1"), at("var"), MULT),
                lambda: combine("quadratic1", at("w1"), 10.0 / 3.0, SUB, at("w1")),
                lambda: combine("y1", at("quadratic1"), 5.0, ADD, at("y0")),
                lambda: combine("square2", at("y1"), REFINED_SQUARE, MULT, at("y1")),
                lambda: binary("w2", at("square2"), at("var"), MULT),
                lambda: (
                    combine("quadratic2", at("w2"), 10.0 / 3.0, SUB, at("w2")),
                    binary("mean_gain", mean, gains, MULT),
                ),
                lambda: combine("y2", at("quadratic2"), 5.0, ADD, at("y1")),
                lambda: (
                    binary("scale", at("y2"), gains, MULT),
                    binary("moved", at("y2"), at("mean_gain"), MULT),
                ),
                offset,
            ]

        def take(u):
            units[u]["linear"] = work.tile([P, UNIT], F32, bufs=7, name="linear_half")
            nc.scalar.copy(out=units[u]["linear"][:], in_=units[u][LINEAR][:])

        def scale_and_offset(u, half, j):
            block = 8 * (u % 2) + 4 * half + j
            return [steps[u // 2][name][:, block : block + 1] for name in ("scale", "offset")]

        def sigmoid(u, j):
            if j == 0:
                units[u]["sigmoid"] = work.tile([P, UNIT], F32, bufs=4, name="sigmoid_half")
            scale, offset = scale_and_offset(u, GATE, j)
            nc.scalar.activation(
                out=units[u]["sigmoid"][:, V * j : V * (j + 1)], in_=units[u][GATE][:, V * j : V * (j + 1)],
                func=SIGMOID, scale=scale, bias=offset,
            )

        def affine(u, j, on_scalar):
            scale, offset = scale_and_offset(u, LINEAR, j)
            block = units[u]["linear"][:, V * j : V * (j + 1)]
            if on_scalar:
                nc.scalar.activation(out=block, in_=block, func=IDENTITY, scale=scale, bias=offset)
            else:
                nc.vector.tensor_scalar(out=block, in0=block, scalar1=scale, scalar2=offset, op0=MULT, op1=ADD)

        def product(u):
            stage, s0, g, c = place(u)
            if stage == 0:
                dst = h_all[:, c : c + 2, s0 : s0 + CHUNK]
            else:
                units[u]["product"] = work.tile([P, UNIT], F32, bufs=7, name="product_tile")
                dst = units[u]["product"][:].rearrange("p (c s) -> p c s", c=2)
            nc.vector.tensor_tensor(
                out=dst,
                in0=units[u]["sigmoid"][:].rearrange("p (c s) -> p c s", c=2),
                in1=units[u]["linear"][:].rearrange("p (c s) -> p c s", c=2),
                op=MULT,
            )
            if stage == 0:
                if u % 2 == 0:
                    steps[u // 2]["slots"] = work.tile([P, 4, CHUNK], F32, name="slots")
                for q in range(2):
                    first = 32 * ((c + q) % 4)
                    nc.sync.dma_start(
                        out=steps[u // 2]["slots"][first : first + 32, :, :].rearrange("p t s -> p (t s)"),
                        in_=h_all[:, c + q, s0 : s0 + CHUNK],
                    )

        def interleave(step):
            steps[step]["grouped"] = work.tile([P, CHUNK, 4], BF16, align_bytes=64, name="grouped")
            nc.scalar.copy(out=steps[step]["grouped"][:], in_=steps[step]["slots"][:].rearrange("p t s -> p s t"))

        def quantise(step):
            stage, s0, g, c = place(2 * step)
            nc.vector.quantize_mx(
                out=h_codes[:, g, s0 : s0 + CHUNK].bitcast(FP8X4),
                scales=h_scales[:, g, s0 : s0 + CHUNK],
                in_=steps[step]["grouped"][:].rearrange("p s t -> p (s t)"),
            )

        def skip_term(u, q, on_scalar):
            stage, s0, g, c = place(u)
            if q == 0:
                units[u]["skip"] = work.tile([P, UNIT], F32, bufs=7, name="skip_tile")
            dst = units[u]["skip"][:, CHUNK * q : CHUNK * (q + 1)]
            src, factor = h_all[:, c + q, s0 : s0 + CHUNK], skip_factor[:, c + q : c + q + 1]
            if on_scalar:
                nc.scalar.activation(out=dst, in_=src, func=COPY, scale=factor)
            else:
                nc.vector.tensor_scalar_mul(dst, src, factor)

        def turn(u, at_end=False):
            if at_end:
                bank = psum.tile([P, UNIT], F32, tag="gate", name="turned_bank")
            else:
                bank = psum.tile([P, UNIT], F32, tag="turned", bufs=1, name="turned_bank")
            units[u]["turned"] = bank
            for v in range(2):
                for q in range(2):
                    block = slice(CHUNK * q + V * v, CHUNK * q + V * (v + 1))
                    for name in ("product", "skip"):
                        nc.tensor.matmul(
                            bank[:, P * (2 * v + q) : P * (2 * v + q + 1)],
                            lhsT=units[u][name][:, block],
                            rhs=ident[:],
                            start=(name == "product"),
                            stop=(name == "skip"),
                            is_transpose=True,
                        )

        def leave(u, on_scalar=True):
            stage, s0, g, c = place(u)
            turned = units[u]["turned"][:].rearrange("p (v c) -> p v c", v=2)
            result = work.tile([P, UNIT], F32, bufs=6, name="result")
            rows = result[:].rearrange("p (v c) -> p v c", v=2)
            column = P * c % D
            if g == 0:
                nc.vector.scalar_tensor_tensor(
                    out=rows, in0=turned, scalar=0.0,
                    in1=d_tile[:, s0 // V : s0 // V + 2, column : column + 2 * P],
                    op0=MAX, op1=ADD,
                )
            elif on_scalar:
                nc.scalar.copy(out=rows, in_=turned)
            else:
                nc.vector.tensor_copy(out=rows, in_=turned)
            nc.sync.dma_start(
                out=(out_0, out_1)[g][s0 : s0 + CHUNK, column : column + 2 * P].rearrange("(v s) c -> s v c", s=V),
                in_=rows,
            )

        def issue(w, item, on_scalar):
            name, numbers = item.split()[0], [int(x) for x in item.split() if x in ("0", "1", "2", "3")]
            half = GATE if "gate" in item else LINEAR
            unit = numbers[0] if numbers else 0
            now, soon, before, out = [2 * (w + lag) + unit for lag in (0, 1, -2, -3)]
            if name == "stats":
                statistics(now, half, numbers[1])
            elif name == "take":
                take(now)
            elif name == "late":
                multiply(now, LINEAR)
            elif name == "matmul" and soon < 2 * STEPS:
                if half == GATE or unit == 0 or w + 1 < TURN_FROM:
                    multiply(soon, half)
            elif name == "sigmoid" and before >= 0:
                sigmoid(before, numbers[1])
            elif name == "affine" and before >= 0:
                for j in range(2 * numbers[1], 2 * numbers[1] + 2):
                    affine(before, j, on_scalar)
            elif name == "product" and before >= 0:
                product(before)
            elif name == "skip" and before >= 2 * STAGE_STEPS:
                skip_term(before, numbers[1], on_scalar)
            elif name == "interleave" and 0 <= w - 3 < STAGE_STEPS:
                interleave(w - 3)
            elif name == "quantise" and 0 <= w - 4 < STAGE_STEPS:
                quantise(w - 4)
            elif name == "turn" and out >= 2 * STAGE_STEPS:
                turn(out)
            elif name == "leave" and out >= 2 * STAGE_STEPS:
                leave(out)
            elif name == "sqrt":
                nc.scalar.activation(out=one_column[:], in_=one_column[:], func=SQRT)

        spread_vectors(0, turn_vectors(0))
        for u in of_step(0):
            multiply(u, LINEAR)
            multiply(u, GATE)
        for w in range(STEPS):
            between = levels(w - 1) if w else []
            for r, row in enumerate(window_order(w)):
                for level in between[r : r + 1]:
                    level()
                for engine, items in enumerate(row):
                    for item in items.split(", "):
                        if item:
                            issue(w, item, engine == 0)
                if w == 2 and r == 1:
                    load_vector_rows(1, (gain2, shift2, skip))
                if w == 4 and r == 2:
                    vector_bank = turn_vectors(1)
                if w == 4 and r == 9:
                    spread_vectors(1, vector_bank)

        last = STEPS - 1
        steps[last]["root"] = work.tile([P, BLOCKS], F32, name="root")
        nc.scalar.activation(
            out=steps[last]["root"][:], in_=moments(last)[1], func=SQRT, scale=1.0 / V, bias=EPS
        )
        nc.scalar.activation(out=one_column[:], in_=one_column[:], func=SIGMOID)
        between = levels(last, rooted=True)
        for u in of_step(last - 1):
            for j in range(4):
                sigmoid(u, j)
        for i, u in enumerate(of_step(last - 1)):
            for j in range(4):
                affine(u, j, False)
            between[2 * i]()
            for q in range(2):
                skip_term(u, q, False)
            between[2 * i + 1]()
        for u in of_step(last):
            for j in range(4):
                sigmoid(u, j)
        for u in of_step(last):
            for q in range(2):
                skip_term(u, q, False)
        for u in of_step(last - 2):
            for q in range(2):
                skip_term(u, q, True)
        for u in of_step(last - 1):
            product(u)
            turn(u, at_end=True)
        for u, earlier in zip(of_step(last), of_step(last - 1)):
            for j in range(4):
                affine(u, j, False)
            product(u)
            turn(u, at_end=True)
            leave(earlier)
        for u in of_step(last - 2):
            turn(u, at_end=True)
        for step in (last, last - 2):
            for i, u in enumerate(of_step(step)):
                leave(u, on_scalar=(i == 0))
